import numpy as np, ml_dtypes
CORES = [10,34,74,98]
N = 4
BF = ml_dtypes.bfloat16
W, S, M, CAP, RO, DX = 8192, 1024, 8, 96, 3, 2
def places(g, w, k):
    u = np.add.reduce(w[..., :, None] * g, axis=-2) & 4095
    return ((u * u >> 5)[..., None, :] + k[..., :, None] * u[..., None, :]) & (W - 1)
def parts(rng):
    return (rng.integers(0, 256, (N, 8, 16, W), dtype=np.int32), rng.integers(0, 256, (N, 8, 16, S)), rng.integers(0, 256, (N, 8, 16, RO)),
            rng.integers(0, 3969, (N, 8, M)), rng.integers(620, 1000, (N, 8)))
def pack(x, g, w, k, t):
    return {"xs": x.reshape(N, 128, W).astype(np.float32).astype(BF), "gd": g.reshape(N, 128, S).astype(np.float32).astype(BF), "wt": w.reshape(N, 128, RO).astype(np.int32),
            "km": np.repeat(k, 16, axis=1).astype(np.int32), "th": np.repeat(t, 16, axis=1)[:, :, None].astype(np.int32)}
def plant(x, g, j, c, i, d):
    v = 255 - g[:, j]; n = np.arange(len(j)); a = v[i, n]
    v[i, n] = np.where(a < 128, a + d, a - d); x[:, c] = v
def lone(rng, x, g, w, k, s0, s1, lo, hi):
    c = places(g, w, k)[:, s0:s1]; m, j = np.nonzero((c >= lo) & (c < hi))
    if len(m):
        i = int(rng.integers(0, len(m))); x[:, c[m[i], j[i]]] = 255 - g[:, s0 + j[i]]
def setup_inputs(rng):
    x, g, w, k, t = parts(rng); h = rng.integers(0, 8)
    t[0, h] = 995; t[1, h] = 620; t[DX, h] = 620
    return pack(x, g, w, k, t)
def setup_inputs_room(rng):
    x, g, w, k, t = parts(rng); t = rng.integers(60, 129, (N, 8)); k = np.minimum(k | 1, 3967)
    for q in range(N):
        room = rng.permutation(np.array([0, 1, CAP - 1, CAP, CAP + 1, 2 * CAP, 0, CAP]))
        for h in range(8):
            c = places(g[q, h], w[q, h, :, 0], k[q, h])[rng.integers(0, M, S), np.arange(S)]
            o = rng.permutation(S); o = o[c[o] < W - 96]; first = np.unique(c[o], return_index=True)[1]
            o = o[np.sort(first)][:int(room[h])]; n = len(o)
            plant(x[q, h], g[q, h], o, c[o], rng.integers(0, 16, n), rng.integers(0, t[q, h], n))
    return pack(x, g, w, k, t)
def setup_inputs_ties(rng):
    x, g, w, k, t = parts(rng)
    w[:, :, 2, 0] = w[:, :, 1, 0]; g[:, :, 1] = np.minimum(g[:, :, 1], 254); g[:, :, 2] = np.maximum(g[:, :, 2], 1)
    for q in range(N):
        for h in (0, 2, 4, 6):
            n = int(rng.choice(np.array([CAP // 4, CAP // 2, CAP]))); t[q, h] = 3 if h == 2 * (q % 4) else rng.integers(1, 4)
            o = rng.permutation(S); a = np.minimum(o[:n], o[n:2 * n]); b = np.maximum(o[:n], o[n:2 * n]); e = o[2 * n:3 * n]
            kd = rng.integers(0, 4, n); kd[:4] = np.arange(4); s = (kd > 0).astype(np.int64)
            v = g[q, h][:, a].copy(); v[1] += s; v[2] -= s; g[q, h][:, b] = v
            c = places(g[q, h], w[q, h, :, 0], k[q, h])
            ca = c[rng.integers(0, M, n), a]; m = rng.integers(0, M, n); c1 = c[m, e]; c2 = c[(m + rng.integers(1, M, n)) % M, e]
            al = np.concatenate([ca, c1, c2]); one = np.bincount(al, minlength=W)[al] == 1
            pa = one[:n] & (ca < W - 96); pe = one[n:2 * n] & one[2 * n:]
            v = 255 - g[q, h][:, a]; v[1] -= ((kd == 1) | (kd == 2)).astype(np.int64); v[2] += (kd == 1).astype(np.int64); x[q, h][:, ca[pa]] = v[:, pa]
            i = rng.integers(0, 16, n); d = rng.integers(0, t[q, h], n)
            plant(x[q, h], g[q, h], e[pe], c1[pe], i[pe], d[pe]); plant(x[q, h], g[q, h], e[pe], c2[pe], i[pe], d[pe])
    a = int(rng.integers(0, S // 4)); b = a + int(rng.integers(1, S // 4))
    w[:, 1, :, 0] = 0; w[:, 1, 0, 0] = 1; k[:, 1, 0] = 0; k[:, 1, 1] = 3; t[:, 1] = 20
    g[:, 1, :, b] = g[:, 1, :, a].copy(); g[:, 1, 0, a] = 32; g[:, 1, 0, b] = 64
    x[:, 1, :, 128] = 255 - g[:, 1, :, a]; x[:, 1, 0, 128] = 207
    return pack(x, g, w, k, t)
def setup_inputs_ends(rng):
    x, g, w, k, t = parts(rng); o = rng.permutation(8); w[:, :, 0, 0] |= 1
    low = rng.integers(0, 192, (N, 4, W)); few = rng.integers(0, 64, (N, W)) == 0
    x[:, o[0], 0] = low[:, 0]; x[:, o[1], 0] = rng.integers(192, 256, (N, W))
    x[:, o[2], 0] = low[:, 1]; x[:, o[2], 0, 0] = 192; x[::2, o[2], 0, W - 1] = 255
    x[1::2, o[2], 0, W - 40] = 192; x[1::2, o[2], 0, W - 20] = 192
    x[:, o[3], 0, W // 2:] = low[:, 2, W // 2:]; x[:, o[4], 0] = np.where(few, 192, low[:, 3])
    x[:, o[6], 0, W - 81:] = low[:, 0, W - 81:]; x[:, o[7], 0, W - 81:] = low[:, 1, W - 81:]; x[:, o[7], 0, W - 4] = 192
    t[::2, o[0]] = 4080; t[1::2, o[0]] = 4; t[1::2, o[2]] = 4
    for q in range(1, N, 2):
        lone(rng, x[q, o[0]], g[q, o[0]], w[q, o[0], :, 0], k[q, o[0]], 0, S // 4, W // 2, W - 96)
        lone(rng, x[q, o[0]], g[q, o[0]], w[q, o[0], :, 1], k[q, o[0]], S // 4, S - 3 * CAP, 0, W // 4)
        lone(rng, x[q, o[2]], g[q, o[2]], w[q, o[2], :, 0], k[q, o[2]], 0, S, 0, W // 4)
    for q in range(N):
        for h in o[5:]:
            u = np.add.reduce(w[q, h, :, 0][:, None] * g[q, h], axis=0) & 4095; used = []
            for m, c in enumerate((W - 97, W - 96, 0)):
                for j in range(S):
                    if u[j] & 1 and j not in used:
                        v = int(u[j]); kk = (c - (v * v >> 5)) * pow(v, -1, W) % W
                        if kk <= 3968:
                            k[q, h, m] = kk; used.append(j)
                            plant(x[q, h], g[q, h], np.array([j]), np.array([c]), np.array([3 + m]), np.array([m])); break
    return pack(x, g, w, k, t)
def setup_inputs_alike(rng):
    x, g, w, k, t = parts(rng); o = rng.permutation(8)
    g[:, o[0]] = g[:, o[0], :, :1].copy()
    for q in range(N):
        c = places(g[q, o[0]], w[q, o[0], :, 0], k[q, o[0]])[:, 0]; m = np.flatnonzero(c < W - 96)[:1]
        plant(x[q, o[0]], g[q, o[0]], np.zeros(len(m), np.int64), c[m], m, np.full(len(m), 3))
    w[:, o[1]] = 0
    for q in range(N):
        e = np.arange(1, CAP + 1); d = np.append(e[::-1] if q % 2 == 0 else e, 0); n = np.arange(CAP + 1); i = rng.integers(0, 16, CAP + 1)
        v = np.repeat(255 - x[q, o[1], :, :1], CAP + 1, axis=1); a = v[i, n]
        v[i, n] = np.where(a < 128, a + d, a - d); g[q, o[1], :, :CAP + 1] = v
    k[:, o[2]] = k[:, o[2], :1].copy()
    g[:, o[3]] = g[:, o[3]][:, :, rng.integers(0, 4, S)]
    b = x[:, o[4], :, :8].copy(); b[:, 0, 0] = 200
    x[:, o[4]] = b[:, :, rng.integers(0, 8, W)]; g[:, o[4]] = 255 - b[:, :, rng.integers(0, 8, S)]
    k[:, o[5]] = rng.choice(np.array([0, 1, 3968]), (N, M))
    x[:, o[6]] = 255 * rng.integers(0, 2, (N, 16, W)); g[:, o[6]] = 255 * rng.integers(0, 2, (N, 16, S))
    w[:, o[7], :, 0] = 0; w[:, o[7], 0, 0] = 1; k[:, o[7]] = rng.integers(0, 8, (N, M)); t[:, o[7]] = 4080
    g[:, o[7], 0] = np.minimum(g[:, o[7], 0], 254); g[:, o[7], 0, S - 1] = 255
    for q in range(N):
        c = int(places(g[q, o[7]], w[q, o[7], :, 0], k[q, o[7]])[0, S - 1]); x[q, o[7], :, c] = 255 - g[q, o[7], :, S - 1]
    return pack(x, g, w, k, t)
def setup_inputs_spread(rng):
    x, g, w, k, t = parts(rng)
    def uneven(n):
        v = np.minimum((np.exp2(8 * rng.random((N, 8, 1, n))) * rng.random((N, 8, 16, n))).astype(np.int64), 255)
        return np.where(rng.random((N, 8, 1, n)) < 0.5, v, 255 - v)
    x = uneven(W); g = uneven(S)
    w = np.minimum(np.exp2(8 * rng.random(w.shape)).astype(np.int64), 255); k = np.minimum(np.exp2(12 * rng.random(k.shape)).astype(np.int64), 3968)
    t = np.minimum(np.maximum(np.exp2(12 * rng.random((N, 8))).astype(np.int64), 1), 4080); t[:, rng.integers(0, 8)] = rng.integers(1500, 2500, N)
    return pack(x, g, w, k, t)
def check_inputs(d):
    bad = []
    for n, lo, hi in (("xs", 0, 255), ("gd", 0, 255), ("wt", 0, 255), ("km", 0, 3968), ("th", 1, 4080)):
        a = np.asarray(d[n]).astype(np.float64)
        if not np.all((a >= lo) & (a <= hi) & (np.floor(a) == a)): bad.append("range of " + n)
    for n in ("km", "th"):
        a = np.asarray(d[n]).reshape(N, 8, 16, -1)
        if np.any(a != a[:, :, :1]): bad.append("rows of a group alike in " + n)
    return bad
def reference(xs, gd, wt, km, th):
    x = xs.astype(np.float32).astype(np.int32).reshape(N, 8, 16, W); g = gd.astype(np.float32).astype(np.int32).reshape(N, 8, 16, S)
    w = wt.astype(np.int64).reshape(N, 8, 16, RO); k = km.astype(np.int64).reshape(N, 8, 16, M)[:, :, 0]; t = th.astype(np.int64).reshape(N, 8, 16)[:, :, 0]
    log = np.zeros((N, 8, W), np.int64); place = np.arange(W); slot = np.arange(S); rows = np.arange(8)[:, None]
    for rnd in range(RO):
        cuts = []; gives = []; nx = []
        for a in range(N):
            c = places(g[a], w[a, :, :, rnd], k[a])
            v = np.take_along_axis(x[a], c.reshape(8, 1, M * S), 2).reshape(8, 16, M, S)
            D = np.add.reduce(np.abs(g[a][:, :, None, :] + v - 255), axis=1)
            m = np.argmin(D, axis=1)[:, None]
            D = np.take_along_axis(D, m, 1)[:, 0].astype(np.int64); c = np.take_along_axis(c, m, 1)[:, 0]
            fit = (D < t[a][:, None]) & (c < W - 96)
            cand = fit & (np.add.accumulate(fit.astype(np.int64), axis=1) <= CAP)
            key = D * S + slot; low = np.full((8, W), 2 ** 40, np.int64)
            np.minimum.at(low, (rows, c), np.where(cand, key, 2 ** 40))
            cut = cand & (np.take_along_axis(low, c, 1) == key)
            ok = (x[a][:, 0] >= 192) & (x[a][:, 0] <= 255)
            U = np.minimum.accumulate(np.where(ok, place, W - 1)[:, ::-1], axis=1)[:, ::-1]
            e1 = np.take_along_axis(U, np.minimum(c + 16, W - 1), 1); e2 = np.take_along_axis(U, np.minimum(e1 + 8, W - 1), 1)
            gives.append([np.maximum(255 - np.take_along_axis(x[a], e[:, None, :], 2), 0) for e in (np.minimum(c + 10, W - 1), e1, e2)])
            reach = np.full((8, W), -1, np.int64); np.maximum.at(reach, (rows, c), np.where(cut, e2, -1))
            gone = np.maximum.accumulate(reach, axis=1) >= place
            log[a] = np.where(gone & (log[a] == 0), rnd + 1, log[a])
            nx.append(np.where(gone[:, None, :], np.int32(512), x[a])); cuts.append(cut)
        ng = []
        for a in range(N):
            p, q = a ^ 1, a ^ DX
            every = np.concatenate([gives[p][0], gives[q][1], gives[q][2], g[a], g[a]], axis=2)
            there = np.concatenate([cuts[p], cuts[q], cuts[q], ~cuts[a], cuts[a]], axis=1)
            o = np.argsort(~there, axis=1, kind="stable")[:, :S]
            ng.append(np.take_along_axis(every, o[:, None, :], 2))
        x = np.stack(nx); g = np.stack(ng)
    return {"yg": g.reshape(N, 128, S).astype(np.float32).astype(BF), "yc": log.astype(np.float32)}

@@ -1,0 +1,505 @@
+from concourse.bass import DstId, RemoteDMATransfer
+from concourse.mybir import AluOpType as O, ActivationFunctionType as AF, AxisListType
+
+W, S, M, CAP, RO = 8192, 1024, 8, 96, 3
+BIG = 16384.0
+QT0 = 2048
+TW = QT0 + 2 * CAP
+GW = S + TW
+
+F32, B16, I32, U16 = "float32", "bfloat16", "int32", "uint16"
+_OWN = {
+    "X": (W, B16), "FW": (W + CAP, F32), "G0": (GW, B16), "G1": (GW, B16), "X0": (512, B16), "CW": (TW, F32),
+    "wti": (3, I32), "kmi": (8, I32), "thi": (1, I32), "LW": (512, F32), "U2": (512, F32), "YC": (512, F32),
+    "UL": (512, F32), "NO": (512, F32), "PL": (512, F32), "D0": (S, F32), "D1": (S, F32), "C": (512, I32), "OFF": (512, U16),
+}
+for _r in range(RO):
+    _OWN.update({"SI%d" % _r: (8, F32), "SP%d" % _r: (96, B16), "ST%d" % _r: (192, B16), "RI%d" % _r: (8, F32), "RJ%d" % _r: (8, F32), "Z%d" % _r: (288 + S, B16)})
+_PART = {
+    F32: {"wtf": 3, "kmf": 8, "th16": 1, "one": 128, "GB": 128, "GBt": 128, "GB8": 128, "GB32": 128, "B0": 128, "ID": 128, "IDB": 128, "USf": 128,
+          "PI": 1, "P512": 1, "P513": 1, "P5K": 1, "CB": 16, "QM": 96, "MW": 96, "RST": 96, "Q0": 96, "Q1": 96, "QT": 96, "CDF": 96, "BI": 64, "QB0": 6, "QB": 6,
+          "i16": 16, "I16": 16, "LM": 16, "PL0": 512, "NEG": 512, "gwA": 8, "gwB": 8, "Uf": 64, "KM": 64, "F0": 64, "PW": 72, "LWn": 72, "BQ": 6, "OH": 96,
+          "LG": 96, "KG": 96, "WL": 96, "SL": 96, "INV": 96, "CG": 96, "WK": 96, "SK": 96, "WC": 96, "SC": 96, "EG": 96, "EG2": 96, "W1": 96, "S1": 96,
+          "W2": 96, "S2": 96, "KB": 576, "CR": 96, "CUT": 96, "NCQ": 96, "RK": 96, "CD": 96, "WD": 96, "SD": 96, "WN": 96, "SN": 96, "LEN": 96, "ZR": 96,
+          "M1": 96, "M2": 96, "RD": 1, "IN": 1, "T1": 6, "T2": 6, "BIF": 12, "HX": 72, "IX": 64, "SLf": 64, "NT1": 1, "NT2": 1, "ST": 512, "OF": 16, "FM": 16, "UI": 1},
+    B16: {"oneb": 128, "GBb": 128, "GBK": 128, "nUS": 128, "IDb": 128, "IDK": 128, "nIDb": 128, "ID2b": 128, "ID3b": 128, "nIDBb": 128, "nB02": 128,
+          "it0": 128, "it1": 128, "IT2": 128, "ib": 64, "SLh": 64, "SLi": 64, "SEL": 2048, "WSA": 2048, "WSB": 2048, "FL": 512, "XG": S, "A0": S, "A1": S, "A2": S,
+          "FIT": 64, "CS": 64, "JK": 384, "INVb": 96, "KL": 576, "EA": 384, "EB": 384, "TA": 768, "GQ": 96, "PG": 96, "PN": 96, "TG": 192, "TN": 192,
+          "F1": 64, "F2": 64, "F3": 64, "SG0": 512, "SG1": 512, "SG2": 512, "N1": 512, "N2": 512},
+    I32: {"pi": 1, "pi2": 1, "Ui": 64, "Um": 64, "UU": 64, "FQ": 64, "CA": 512, "KMi": 64, "PAR": 64, "MX": 64, "KD": 72, "XA": 6, "XI": 6, "VV": 6, "BII": 12},
+    U16: {"BQo": 6, "LO": 6, "UO": 6, "UO2": 6, "PO": 6, "TO": 12, "CDu": 6, "ROu": 6, "SQ": 6, "IXu": 64, "FX": 64},
+}
+_AT, SCRATCH = {}, {n: ("sbuf", [128, c], d) for n, (c, d) in _OWN.items()}
+for _d, _n in ((F32, "SF"), (B16, "SB"), (I32, "SJ"), (U16, "SU")):
+    _c = 0
+    for _k, _w in _PART[_d].items():
+        _AT[_k] = (_n, _c, _w)
+        _c += -(-_w // 16) * 16
+    SCRATCH[_n] = ("sbuf", [128, _c], _d)
+_PS = ["pA", "pB", "pM", "pN", "pK0", "pK1", "pD0", "pD1"]
+SCRATCH.update({n: ("psum", [128, 512], F32) for n in _PS})
+SEMAPHORES = ["sv", "ss", "st", "sg", "loc"] + ["a%s%d" % (k, r) for k in "ijpt" for r in range(RO)] + ["d%d" % k for k in range(30)]
+
+
+def _queues(g, T):
+    Q = {"v": g.vector, "s": g.scalar, "t": g.tensor, "g": g, "y": g.sync}
+    ENG = {"v": "sv", "s": "ss", "t": "st", "g": "sg"}
+    cnt, seen, acc, no = {}, {q: {} for q in Q}, {}, [0, 0]
+
+    def A(n, a=0, b=None, s=1, rows=None):
+        m, off, w = _AT[n] if n in _AT else (n, 0, T[n].shape[1])
+        b = w if b is None else b
+        a, b, t = a + off, b + off, T[m]
+        if rows is not None:
+            ap = t[rows, a:b]
+        elif s < 0:
+            ap = t[:, ::-1]
+        elif s > 1:
+            ap = t[:, a:b:s]
+        else:
+            ap = t[:, a:b]
+        return (ap, ((m, a, b, abs(s)),), ())
+
+    def X(ap):
+        return (ap, (), ())
+
+    def IND(win, off):
+        return (win[0].indirect(off[0]), win[1], off[1])
+
+    def need(q, outs, ins, chain=False):
+        deps = []
+        for w, regs in ((True, outs), (False, ins)):
+            for (n, a, b, s) in regs:
+                ps = n in _PS
+                for rec in acc.get(n, ()):
+                    rw, rq, sem, val, ra, rb, rs, clk, k = rec
+                    if not (w or rw or (ps and rq != q)):
+                        continue
+                    if not (ps and rq != q):
+                        if b <= ra or rb <= a or (s == rs and s > 1 and (a - ra) % s):
+                            continue
+                        if rq == q and chain and w:
+                            continue
+                    deps.append((k, sem, val, clk))
+        deps.sort(key=lambda d: -d[0])
+        for k, sem, val, clk in deps:
+            if seen[q].get(sem, 0) >= val:
+                continue
+            Q[q].wait_ge(T.sem[sem], val)
+            for s2, v2 in clk.items():
+                if seen[q].get(s2, 0) < v2:
+                    seen[q][s2] = v2
+            seen[q][sem] = max(val, seen[q].get(sem, 0))
+
+    def note(q, sem, val, clk, outs, ins):
+        no[0] += 1
+        for w, regs in ((True, outs), (False, ins)):
+            for (n, a, b, s) in regs:
+                old = acc.get(n, [])
+                if w and s == 1:
+                    old = [x for x in old if not (a <= x[4] and x[5] <= b)]
+                old.append((w, q, sem, val, a, b, s, clk, no[0]))
+                acc[n] = old
+
+    def split(outs, ins):
+        o = [x for p in outs for x in p[1]]
+        i = [x for p in outs for x in p[2]] + [x for p in ins if isinstance(p, tuple) for x in p[1] + p[2]]
+        return o, i
+
+    def run(q, outs, ins, call, chain=False):
+        o, i = split(outs, ins)
+        need(q, o, i, chain)
+        sem = ENG[q]
+        cnt[sem] = cnt.get(sem, 0) + 1
+        call().then_inc(T.sem[sem], 1)
+        clk = dict(seen[q])
+        clk[sem] = cnt[sem]
+        note(q, sem, cnt[sem], clk, o, i)
+
+    def v(x):
+        return x[0] if isinstance(x, tuple) else x
+
+    V, SC, TE = g.vector, g.scalar, g.tensor
+
+    def TT(o, a, b, op):
+        run("v", [o], [a, b], lambda: V.tensor_tensor(out=o[0], in0=a[0], in1=b[0], op=op))
+
+    def TS(o, a, s1, s2, op0, op1=None):
+        if op1 is None:
+            run("v", [o], [a, s1], lambda: V.tensor_scalar(out=o[0], in0=a[0], scalar1=v(s1), scalar2=None, op0=op0))
+        else:
+            run("v", [o], [a, s1, s2], lambda: V.tensor_scalar(out=o[0], in0=a[0], scalar1=v(s1), scalar2=v(s2), op0=op0, op1=op1))
+
+    def TC(o, a):
+        run("v", [o], [a], lambda: V.tensor_copy(out=o[0], in_=a[0]))
+
+    def MS(o, c):
+        run("v", [o], [], lambda: V.memset(o[0], c))
+
+    def RED(o, a, op):
+        run("v", [o], [a], lambda: V.tensor_reduce(out=o[0], in_=a[0], axis=AxisListType.X, op=op))
+
+    def SCAN(o, a, b, init, op0, op1):
+        run("v", [o], [a, b, init], lambda: V.tensor_tensor_scan(out=o[0], data0=a[0], data1=b[0], initial=v(init), op0=op0, op1=op1))
+
+    def ACT(o, a, f, bias=0.0, scale=1.0, acc=None):
+        if acc is None:
+            run("s", [o], [a, bias, scale], lambda: SC.activation(out=o[0], in_=a[0], func=f, bias=v(bias), scale=v(scale)))
+        else:
+            run("s", [o, acc], [a, bias, scale], lambda: SC.activation(out=o[0], in_=a[0], func=f, bias=v(bias), scale=v(scale), accum_out=acc[0]))
+
+    def MM(o, l, r, start, stop):
+        run("t", [o], [l, r], lambda: TE.matmul(o[0], l[0], r[0], start=start, stop=stop), not start)
+
+    def IOTA(o, pat, base, cm):
+        run("g", [o], [], lambda: g.iota(o[0], pat, base, cm, allow_small_or_imprecise_dtypes=True))
+
+    def AFF(o, a, pat, op, base, cm):
+        run("g", [o], [a], lambda: g.affine_select(o[0], a[0], pat, op, 0.0, base, cm))
+
+    def DMA(q, o, a):
+        os_, is_ = split([o], [a])
+        need(q, os_, is_)
+        sem = "d%d" % no[1]
+        no[1] += 1
+        Q[q].dma_start(o[0], a[0]).then_inc(T.sem[sem], 16)
+        cnt[sem] = 16
+        clk = dict(seen[q])
+        clk[sem] = 16
+        note("dma", sem, 16, clk, os_, is_)
+
+    def SEND(srcs, engines, call):
+        o, i = split([], srcs)
+        need("g", o, i)
+        call()
+        cnt["loc"] = cnt.get("loc", 0) + engines
+        note("rem", "loc", cnt["loc"], {}, o, i)
+
+    def LAND(dst, sem, val):
+        cnt[sem] = val
+        note("rem", sem, val, {sem: val}, list(dst[1]), [])
+
+    def END():
+        for sem in cnt:
+            if max(seen[q].get(sem, 0) for q in Q) < cnt[sem]:
+                g.wait_ge(T.sem[sem], cnt[sem])
+
+    return A, X, IND, TT, TS, TC, MS, RED, SCAN, ACT, MM, IOTA, AFF, DMA, SEND, LAND, END
+
+
+def rank_program(g, core, T, topo):
+    rank = T.rank_of(core)
+    if rank is None:
+        return
+    A, XT, IND, TT, TS, TC, MS, RED, SCAN, ACT, MM, IOTA, AFF, DMA, SEND, LAND, END = _queues(g, T)
+    CP, RL = AF.Copy, AF.Relu
+    q6 = (15, 96, 16)
+
+    DMA("y", A("G0", 0, S), XT(T.gd[:, :]))
+    DMA("s", A("wti"), XT(T.wt[:, :]))
+    DMA("s", A("kmi"), XT(T.km[:, :]))
+    DMA("s", A("thi"), XT(T.th[:, :]))
+    DMA("s", A("X", W // 2, W), XT(T.xs[:, W // 2:W]))
+    DMA("y", A("X", 0, W // 2), XT(T.xs[:, 0:W // 2]))
+    DMA("y", A("X0"), XT(T.xs[0::16, :]))
+
+    MS(A("one"), 1.0)
+    MS(A("oneb"), 1.0)
+    IOTA(A("pi"), [[0, 1]], 0, 1)
+    AFF(A("GBt"), A("one"), [[-16, 8], [0, 16]], O.is_ge, 0, 1)
+    AFF(A("GB"), A("GBt"), [[16, 8], [0, 16]], O.is_ge, 15, -1)
+    AFF(A("ID"), A("GB"), [[-1, 128]], O.is_equal, 0, 1)
+    MS(A("WSA"), 0.0)
+    for n, c in enumerate((-4080.0, 383.0 * BIG, 255.0, 95.0)):
+        MS(A("CB", n, n + 1), c)
+    TS(A("pi2"), A("pi"), 15, None, O.bitwise_and)
+    TC(A("PI"), A("pi2"))
+    TC(A("wtf"), A("wti"))
+    TC(A("kmf"), A("kmi"))
+    TS(A("gwA"), A("GB", 0, 128, 16), A("wtf", 0, 1), None, O.mult)
+    MS(A("SEL"), 0.0)
+
+    def spread(dst, src, step):
+        for h in range(8):
+            ACT(A(dst, 16 * h, 16 * h + 129 * 15 + 1, 129), A("oneb", 0, 16), CP, scale=A(src, step * h, step * h + 1))
+    spread("WSA", "gwA", 1)
+
+    def lists(r):
+        G, WS = "G%d" % (r % 2), ("WSA", "WSB")[r % 2]
+        for i in range(16):
+            MM(A("pA", 0, 64), A(WS, 128 * i, 128 * i + 128), A(G, i, S, 16), i == 0, i == 15)
+        TC(A("Ui"), A("pA", 0, 64))
+        TS(A("Um"), A("Ui"), 4095, None, O.bitwise_and)
+        TC(A("Uf"), A("Um"))
+        for m in range(M):
+            ACT(A(("pB", "pM")[m // 4], 64 * (m % 4), 64 * (m % 4) + 64), A("Uf"), CP, scale=A("kmf", m, m + 1))
+        TT(A("UU"), A("Um"), A("Um"), O.mult)
+        TS(A("FQ"), A("UU"), 5, None, O.arith_shift_right)
+        for h in range(2):
+            for m in range(4 * h, 4 * h + 4):
+                TT(A("CA", 64 * m, 64 * m + 64), A(("pB", "pM")[h], 64 * (m % 4), 64 * (m % 4) + 64), A("FQ"), O.add)
+            TS(A("C", 256 * h, 256 * h + 256), A("CA", 256 * h, 256 * h + 256), W - 1, None, O.bitwise_and)
+            TC(A("OFF", 256 * h, 256 * h + 256), A("C", 256 * h, 256 * h + 256))
+            if h == 0 and r:
+                ACT(A("XG"), IND(A("X"), A("OFF", 0, 64)), CP)
+
+    KB3 = ("pK0", "pK1", "pN")
+
+    def scores(r):
+        G = "G%d" % (r % 2)
+        for h in range(2):
+            MM(A("pD%d" % h), A("IDb"), A("XG", 512 * h, 512 * h + 512), True, False)
+            MM(A("pD%d" % h), A("IDb"), A(G, 512 * h, 512 * h + 512), False, True)
+
+        def flag(m):
+            TS(A("FL", 64 * m, 64 * m + 64), A("C", 64 * m, 64 * m + 64), W - 96, 2 * m, O.is_ge, O.add)
+
+        def keys(m):
+            k = KB3[m % 3]
+            for i in range(16):
+                MM(A(k, 0, 64), A("SEL", 128 * i, 128 * i + 128), A("A%d" % (m % 3), i, S, 16), i == 0, False)
+            MM(A(k, 0, 64), A("IDb"), A("FL", 64 * m, 64 * m + 64), False, True)
+
+        def least(m):
+            if m == 0:
+                TC(A("KM"), A(KB3[0], 0, 64))
+            elif m > 0:
+                TT(A("KM"), A(KB3[m % 3], 0, 64), A("KM"), O.min)
+        for h in range(2):
+            ACT(A("A0", 512 * h, 512 * h + 512), A("pD%d" % h), AF.Abs, bias=A("CB", 0, 1), scale=16.0)
+        for m in range(1, M):
+            for h in range(2 if m == M - 1 else 1):
+                n = S // 2 if m == M - 1 else S
+                a, b = n * h, n * h + n
+                TT(A("D%d" % (m % 2), a, b), IND(A("X"), A("OFF", 64 * m + a // 16, 64 * m + b // 16)), A(G, a, b), O.add)
+                ACT(A("A%d" % (m % 3), a, b), A("D%d" % (m % 2), a, b), AF.Abs, bias=A("CB", 0, 1), scale=16.0)
+            if m == 3:
+                ACT(A("NO"), A("X0"), RL, bias=A("CB", 1, 2), scale=-2 * BIG)
+            if m == 1:
+                flag(0)
+                keys(0)
+            flag(m)
+            keys(m)
+            least(m - 2)
+        least(M - 2)
+        utable()
+        least(M - 1)
+
+    def wrap(dst, src, tmp):
+        TT(A(tmp), src, A("MW"), O.mult)
+        SCAN(A(dst), A("RST"), A(tmp), 0.0, O.mult, O.add)
+
+    def utable():
+        SCAN(A("UL", s=-1), A("NO", s=-1), A("PL", s=-1), float(W + 1), O.min, O.max)
+        TS(A("OF"), A("I16"), A("UL", 0, 1), None, O.mult)
+        MM(A("pD0", 0, 16), A("GB"), A("OF"), True, True)
+        TT(A("FM"), A("pD0", 0, 16), A("LM"), O.max)
+        RED(A("UI"), A("FM"), O.min)
+        TS(A("U2"), A("UL"), A("UI"), None, O.min)
+        DMA("y", A("FW", 0, W, rows=slice(0, 128, 16)), A("U2"))
+
+    lists(0)
+    IOTA(A("QM"), [[0, 6], [1, 16]], 0, 0)
+    AFF(A("B0"), A("GB"), [[-16, 8], [0, 16]], O.is_equal, 0, 1)
+    AFF(A("USf"), A("GB"), [[-1, 128]], O.is_gt, 0, 1)
+    IOTA(A("PL0"), [[1, 512]], 2, 0)
+    IOTA(A("QB0"), [[16, 6]], 0, 0)
+    IOTA(A("BI"), [[1, 64]], 0, 0)
+    IOTA(A("i16"), [[1, 16]], 0, 0)
+    IOTA(A("it0"), [[0, 8], [1, 16]], 1, 0)
+    for n, c, base in (("Q0", 96, 0), ("Q1", 96, 1), ("QT", 96, QT0), ("CDF", 96, W + 1), ("ib", 64, 0)):
+        IOTA(A(n), [[1, c]], base, 0)
+    IOTA(A("SLh"), [[16, 64]], 0, 0)
+    IOTA(A("FW"), [[0, W + CAP]], 0, 0)
+    for n, c, base in (("KD", 72, 0), ("PW", 72, -1), ("LWn", 72, 0), ("HX", 72, 0), ("ZR", 96, 0), ("NEG", 512, -1), ("WSB", 2048, 0), ("SI0", 8, 0), ("SI1", 8, 0), ("SI2", 8, 0)):
+        IOTA(A(n), [[0, c]], base, 0)
+    for n in ("G0", "G1"):
+        IOTA(A(n, S, S + CAP), [[0, CAP]], 0, 0)
+    spread("SEL", "GB", 16)
+    for n, a, c in (("IDb", "ID", 1.0), ("GBb", "GB", 1.0), ("nUS", "USf", -1.0), ("GB32", "GB", 32.0), ("GB8", "GB", 8.0), ("IDB", "ID", BIG)):
+        ACT(A(n), A(a), CP, scale=c)
+    ACT(A("XG"), IND(A("X"), A("OFF", 0, 64)), CP)
+    TS(A("th16"), A("thi"), 16.0, None, O.mult)
+    TS(A("P512"), A("PI"), 512.0, None, O.mult)
+    TS(A("P513"), A("PI"), 512.0, 1.0, O.mult, O.add)
+    TS(A("P5K"), A("P513"), 10000.0, None, O.mult)
+    TS(A("PL"), A("PL0"), A("P512"), None, O.add)
+    TS(A("MW"), A("QM"), A("PI"), None, O.is_equal)
+    TS(A("RST"), A("QM"), 0.0, None, O.is_gt)
+    TS(A("QB"), A("QB0"), A("PI"), 0.5, O.add, O.add)
+    TS(A("CB", 4, 5), A("PI"), 1.0 / 1024, None, O.mult)
+    TS(A("BI"), A("BI"), 1.0 / 32, A("CB", 4, 5), O.mult, O.add)
+    TS(A("I16"), A("i16"), A("PI"), None, O.is_equal)
+    TS(A("LM"), A("i16"), A("PI"), BIG, O.is_le, O.mult)
+    TS(A("SLi"), A("oneb", 0, 64), A("PI"), None, O.mult)
+    TS(A("SLf"), A("SLh"), A("PI"), None, O.add)
+    TT(A("it1"), A("it0"), A("GB"), O.mult)
+    TS(A("IT2"), A("it1"), -1.0, None, O.add)
+    TS(A("gwB"), A("GB", 0, 128, 16), A("wtf", 1, 2), None, O.mult)
+    TS(A("gwA"), A("GB", 0, 128, 16), A("wtf", 2, 3), None, O.mult)
+
+    near, far = T.cores[rank ^ 1], T.cores[rank ^ 2]
+
+    def to(dst, eng, sem, src, out):
+        rid, pid = topo.addr(dst)[0:2]
+        return RemoteDMATransfer(dst_ids=[DstId(rid=rid, pnc=pid)], dma_engine_mask=sum(1 << e for e in eng), remote_sem=T.sem[sem], src=src[0], dst=out[0])
+    en, ef = topo.engines(core, near), topo.engines(core, far)
+    hn = len(en) // 2
+
+    for r in range(RO):
+        last = r == RO - 1
+        G, H = "G%d" % (r % 2), "G%d" % ((r + 1) % 2)
+        SI, SP, STn, RI, RJ, Z, SG = ("%s%d" % (n, r) for n in ("SI", "SP", "ST", "RI", "RJ", "Z", "SG"))
+        if r:
+            lists(r)
+        scores(r)
+        if r == 0:
+            for n, a, c in (("nB02", "B0", -2.0), ("nIDBb", "ID", -BIG), ("nIDb", "ID", -1.0), ("GBK", "GB", BIG), ("IDK", "ID", BIG),
+                            ("ID2b", "ID", 2.0), ("ID3b", "ID", 3.0)):
+                ACT(A(n), A(a), CP, scale=c)
+        TS(A("F0"), A("KM"), A("th16"), None, O.is_lt)
+        TC(A("KMi"), A("KM"))
+        TS(A("PAR"), A("KMi"), 1, None, O.bitwise_and)
+        TT(A("FIT"), A("F0"), A("PAR"), O.is_gt)
+        SCAN(A("CS"), A("one", 0, 64), A("FIT"), 0.0, O.mult, O.add)
+        MM(A("pB", 0, 64), A("GBb"), A("CS"), True, True)
+        MM(A("pM", 0, 64), A("GBb"), A("CS"), True, False)
+        MM(A("pM", 0, 64), A("nUS"), A("FIT"), False, True)
+        MM(A("pN", 0, 64), A("GBb"), A("CS"), True, True)
+        for a in range(6):
+            ACT(A("JK", 64 * a, 64 * a + 64), A("pB", 0, 64), AF.Sign, bias=A("QB", a, a + 1), scale=-1.0, acc=A("BQ", a, a + 1))
+        TS(A("MX"), A("KMi"), 14, None, O.bitwise_and)
+        TT(A("LWn", 0, 64), A("MX"), A("BI"), O.add)
+        TT(A("PW", 0, 64), A("pM", 0, 64), A("FIT"), O.mult)
+        TS(A("KD", 0, 64), A("KMi"), 65520, None, O.bitwise_and)
+        TS(A("INVb"), A("Q0"), A("pN", 63, 64), None, O.is_ge)
+        TS(A("INV"), A("INVb"), 2.0 ** -14, None, O.add)
+        ACT(A("CW", 0, 96), A("CDF"), CP)
+        TS(A("BQo"), A("BQ"), 0.5, 32.0, O.mult, O.add)
+        TT(A("OH"), IND(A("PW"), A("BQo")), A("Q1"), O.is_equal)
+        TT(A("LG"), IND(A("LWn"), A("BQo")), A("OH"), O.mult)
+        MM(A("pA", 0, 96), A("GB32"), A("LG"), True, True)
+        TT(A("KG"), IND(A("KD"), A("BQo")), A("OH"), O.mult)
+        MM(A("pK0", 0, 96), A("GB8"), A("KG"), True, False)
+        MM(A("pK0", 0, 96), A("ID"), A("Q0"), False, True)
+        TS(A("T1"), A("BQ"), 8.0, 512.0, O.mult, O.add)
+        wrap("SL", A("pA", 0, 96), "WL")
+        TC(A("LO"), A("SL", *q6))
+        TT(A("CG"), IND(A("C"), A("LO")), A("OH"), O.mult)
+        MM(A("pA", 0, 96), A("GB"), A("CG"), True, False)
+        MM(A("pA", 0, 96), A("IDB"), A("INV"), False, True)
+        wrap("SK", A("pK0", 0, 96), "WK")
+        TS(A("XA"), A("SL", *q6), 32.0, None, O.mult)
+        TS(A("XI"), A("XA"), 2047, None, O.bitwise_and)
+        TT(A("T2"), A("XI"), A("T1"), O.subtract)
+        wrap("SC", A("pA", 0, 96), "WC")
+        ACT(A("CR"), A("pA", 0, 96), CP)
+        for a in range(6):
+            TS(A("KB", 96 * a, 96 * a + 96), A("pK0", 0, 96), A("SK", 16 * a + 15, 16 * a + 16), A("SC", 16 * a + 15, 16 * a + 16), O.is_gt, O.mult)
+        for a in range(6):
+            TT(A("KL", 96 * a, 96 * a + 96), A("KB", 96 * a, 96 * a + 96), A("pA", 0, 96), O.is_equal)
+            MM(A("pK1", 0, 96), A("GBK"), A("KL", 96 * a, 96 * a + 96), a == 0, False)
+        MM(A("pK1", 0, 96), A("IDK"), A("INVb"), False, True)
+        TC(A("SQ"), A("T2"))
+        ACT(A("GQ"), IND(A(G, 0, S), A("SQ")), CP)
+        TT(A("NCQ"), A("pK1", 0, 96), A("QT"), O.min)
+        TS(A("CUT"), A("NCQ"), 0.5, None, O.is_lt)
+        SCAN(A("RK"), A("one", 0, 96), A("CUT"), -1.0, O.mult, O.add)
+        TT(A("CD"), A("NCQ"), A("RK"), O.add)
+        wrap("SD", A("CD"), "WD")
+        TC(A("CDu"), A("SD", *q6))
+        if not last:
+            spread(("WSB", "WSA")[r], ("gwB", "gwA")[r], 1)
+        ACT(A(SI, 0, 1), A("RK", 95, 96), AF.Identity, bias=A("one", 0, 1))
+        ACT(A(SI, 7, 8), A("RK", 95, 96), AF.Identity, bias=A("CB", 3, 4), scale=-1.0)
+        SEND([A(SI)], 2 * hn, lambda: g.remote_dma_fused([to(near, en[:hn], "ai%d" % r, A(SI), A(RI)), to(far, ef[hn:], "aj%d" % r, A(SI), A(RJ))], local_sem=T.sem["loc"]))
+        TC(IND(A("CW"), A("CDu")), A("CR"))
+        wrap("SN", A("CW", 0, 96), "WN")
+        TS(A("UO"), A("SN", *q6), 15.0, W - 1.0, O.add, O.min)
+        TC(A("EG"), IND(A("FW"), A("UO")))
+        MM(A("pM", 0, 96), A("B0"), A("EG"), True, True)
+        TS(A("PO"), A("SN", *q6), 9.0, W - 1.0, O.add, O.min)
+        ACT(A("PG"), IND(A("X"), A("PO")), CP)
+        ACT(A("PN"), A("PG"), RL, scale=-1.0)
+        MM(A("pD0", 0, 96), A("nIDb"), A("PG"), True, False)
+        MM(A("pD0", 0, 96), A("nB02"), A("PN"), False, True)
+        ACT(A(SP), A("pD0", 0, 96), RL, bias=A("CB", 2, 3))
+        SEND([A(SP)], len(en), lambda: g.remote_dma_fused([to(near, en, "ap%d" % r, A(SP), A(Z, 0, 96))], local_sem=T.sem["loc"]))
+        TT(A("VV"), A("T2"), A("SD", *q6), O.subtract)
+        TS(A("BII", 0, 6), A("VV"), 16383, 4, O.bitwise_and, O.arith_shift_right)
+        wrap("S1", A("pM", 0, 96), "W1")
+        TS(A("UO2"), A("S1", *q6), 6.0, W - 1.0, O.add, O.min)
+        TC(A("EG2"), IND(A("FW"), A("UO2")))
+        MM(A("pN", 0, 96), A("B0"), A("EG2"), True, True)
+        TS(A("TO", 0, 6), A("S1", *q6), -2.0, None, O.add)
+        TS(A("BII", 6, 12), A("VV"), 15, None, O.bitwise_and)
+        TC(A("BIF"), A("BII"))
+        TS(A("ROu"), A("SN", *q6), -1.0, None, O.add)
+        wrap("S2", A("pN", 0, 96), "W2")
+        TS(A("TO", 6, 12), A("S2", *q6), -2.0, None, O.add)
+        ACT(A("TG"), IND(A("X"), A("TO")), CP)
+        ACT(A("TN"), A("TG"), RL, scale=-1.0)
+        MM(A("pD1", 0, 192), A("nIDb"), A("TG"), True, False)
+        MM(A("pD1", 0, 192), A("nB02"), A("TN"), False, True)
+        ACT(A(STn), A("pD1", 0, 192), RL, bias=A("CB", 2, 3))
+        SEND([A(STn)], len(ef), lambda: g.remote_dma_fused([to(far, ef, "at%d" % r, A(STn), A(Z, 96, 288))], local_sem=T.sem["loc"]))
+        LAND(A(RI), "ai%d" % r, hn)
+        LAND(A(RJ), "aj%d" % r, len(ef) - hn)
+        LAND(A(Z, 0, 96), "ap%d" % r, len(en))
+        LAND(A(Z, 96, 288), "at%d" % r, len(ef))
+        TT(A("LEN"), A("pN", 0, 96), A("CW", 0, 96), O.subtract)
+        TC(IND(A("FW"), A("ROu")), A("LEN"))
+        DMA("y", A("LW"), A("FW", 0, W, rows=slice(1, 128, 16)))
+        TC(IND(A(G, S, GW), A("CDu")), A("GQ"))
+        for a in range(6):
+            ACT(A("EA", 64 * a, 64 * a + 64), A("ib"), AF.Abs, bias=A("BIF", a, a + 1), scale=-1.0)
+        ACT(A("EB"), A("EA"), RL, bias=A("one", 0, 1), scale=-1.0)
+        for a in range(6):
+            TS(A("TA", 128 * a, 128 * a + 128), A("IT2"), A("BIF", 6 + a, 7 + a), None, O.is_ge)
+        for a in range(6):
+            MM(A("pB", 0, 64), A("GBb"), A("EB", 64 * a, 64 * a + 64), a == 0, a == 5)
+        MM(A("pA", 0, 64), A("IDb"), A("SLh"), True, False)
+        MM(A("pA", 0, 64), A("IDb"), A("SLi"), False, False)
+        for a in range(6):
+            MM(A("pA", 0, 64), A("TA", 128 * a, 128 * a + 128), A("EB", 64 * a, 64 * a + 64), False, a == 5)
+        ACT(A("M1"), A("CW", 0, 96), RL, bias=A("P5K"), scale=-10000.0)
+        TT(A("M2"), A("pN", 0, 96), A("M1"), O.min)
+        RED(A("RD"), A("M2"), O.max)
+        TS(A("IN"), A("RD"), A("P512"), 0.0, O.subtract, O.max)
+        SCAN(A("HX", 1, 65), A("one", 0, 64), A("pB", 0, 64), 0.0, O.mult, O.add)
+        TT(A("IX"), A("pA", 0, 64), A("HX", 0, 64), O.add)
+        TC(A("IXu"), A("IX"))
+        ACT(A(Z, 288, 288 + S), IND(A(G, 0, S + CAP), A("IXu")), CP)
+        SCAN(A("ST"), A("NEG"), A("LW"), A("IN"), O.add, O.max)
+        ACT(A(SG), A("ST"), AF.Sign)
+        if not last:
+            MM(A("pK0"), A("IDb"), A("X0"), True, False)
+            MM(A("pK0"), A("nIDBb"), A(SG), False, True)
+            ACT(A("X0"), A("pK0"), CP)
+            DMA("y", A("X", 0, W, rows=slice(0, 128, 16)), A("X0"))
+            TC(IND(A("FW"), A("ROu")), A("ZR"))
+        ACT(A("NT1"), A(RI, 0, 1), AF.Identity, bias=A(RJ, 0, 1))
+        ACT(A("NT2"), A("NT1"), AF.Identity, bias=A(RJ, 0, 1))
+        TS(A("F1"), A("SLf"), A(RI, 0, 1), A(RI, 7, 8), O.is_ge, O.mult)
+        TS(A("F2"), A("SLf"), A("NT1"), A(RJ, 7, 8), O.is_ge, O.mult)
+        TS(A("F3"), A("SLf"), A("NT2"), A(RJ, 7, 8), O.is_ge, O.mult)
+        for k, n in enumerate(("SLh", "SLi", "F1", "F2", "F3")):
+            MM(A("pM", 0, 64), A("IDb"), A(n), k == 0, k == 4)
+        TC(A("FX"), A("pM", 0, 64))
+        TC(A(H, 0, S // 2), IND(A(Z), A("FX", 0, 32)))
+        ACT(A(H, S // 2, S), IND(A(Z), A("FX", 32, 64)), CP)
+        if last:
+            DMA("y", XT(T.yg[:, :]), A(H, 0, S))
+        if r:
+            MM(A("pK1"), A("IDb"), A(SG), True, False)
+            MM(A("pK1"), A("nIDb"), A("SG0"), False, r == 1)
+            if r == 2:
+                MM(A("pK1"), A("nIDb"), A("N1"), False, True)
+            ACT(A("N%d" % r), A("pK1"), RL)
+        if last:
+            MM(A("pD0"), A("IDb"), A("SG0"), True, False)
+            MM(A("pD0"), A("ID2b"), A("N1"), False, False)
+            MM(A("pD0"), A("ID3b"), A("N2"), False, True)
+            ACT(A("YC"), A("pD0"), CP)
+            DMA("s", XT(T.yc[:, :]), A("YC"))
+    END()

@@ -3,13 +3,11 @@ from concourse.mybir import AluOpType as O, ActivationFunctionType as AF, AxisLi
 
 W, S, M, CAP, RO = 8192, 1024, 8, 96, 3
 BIG = 16384.0
-QT0 = 2048
-TW = QT0 + 2 * CAP
-GW = S + TW
+FWW = W + 2 * CAP
 
 F32, B16, I32, U16 = "float32", "bfloat16", "int32", "uint16"
 _OWN = {
-    "X": (W, B16), "FW": (W + CAP, F32), "G0": (GW, B16), "G1": (GW, B16), "X0": (512, B16), "CW": (TW, F32),
+    "X": (W, B16), "FW": (FWW, F32), "G0": (S + CAP, B16), "G1": (S + CAP, B16), "X0": (512, B16),
     "wti": (3, I32), "kmi": (8, I32), "thi": (1, I32), "LW": (512, F32), "U2": (512, F32), "YC": (512, F32),
     "UL": (512, F32), "NO": (512, F32), "PL": (512, F32), "D0": (S, F32), "D1": (S, F32), "C": (512, I32), "OFF": (512, U16),
 }
@@ -17,17 +15,17 @@ for _r in range(RO):
     _OWN.update({"SI%d" % _r: (8, F32), "SP%d" % _r: (96, B16), "ST%d" % _r: (192, B16), "RI%d" % _r: (8, F32), "RJ%d" % _r: (8, F32), "Z%d" % _r: (288 + S, B16)})
 _PART = {
     F32: {"wtf": 3, "kmf": 8, "th16": 1, "one": 128, "GB": 128, "GBt": 128, "GB8": 128, "GB32": 128, "B0": 128, "ID": 128, "IDB": 128, "USf": 128,
-          "PI": 1, "P512": 1, "P513": 1, "P5K": 1, "CB": 16, "QM": 96, "MW": 96, "RST": 96, "Q0": 96, "Q1": 96, "QT": 96, "CDF": 96, "BI": 64, "QB0": 6, "QB": 6,
+          "PI": 1, "P512": 1, "P513": 1, "P5K": 1, "CB": 16, "QM": 96, "MW": 96, "RST": 96, "Q0": 96, "Q1": 96, "QT": 96, "NMW": 96, "BI": 64, "QB0": 6, "QB": 6, "QBK": 6, "BK": 6,
           "i16": 16, "I16": 16, "LM": 16, "PL0": 512, "NEG": 512, "gwA": 8, "gwB": 8, "Uf": 64, "KM": 64, "F0": 64, "PW": 72, "LWn": 72, "BQ": 6, "OH": 96,
           "LG": 96, "KG": 96, "WL": 96, "SL": 96, "INV": 96, "CG": 96, "WK": 96, "SK": 96, "WC": 96, "SC": 96, "EG": 96, "EG2": 96, "W1": 96, "S1": 96,
-          "W2": 96, "S2": 96, "KB": 576, "CR": 96, "CUT": 96, "NCQ": 96, "RK": 96, "CD": 96, "WD": 96, "SD": 96, "WN": 96, "SN": 96, "LEN": 96, "ZR": 96,
+          "W2": 96, "S2": 96, "KB": 576, "SGN": 576, "C6": 6, "R6": 6, "CR": 96, "CUT": 96, "NCQ": 96, "RK": 96, "CD": 96, "WD": 96, "SD": 96, "LEN": 96, "ZR": 96,
           "M1": 96, "M2": 96, "RD": 1, "IN": 1, "T1": 6, "T2": 6, "BIF": 12, "HX": 72, "IX": 64, "SLf": 64, "NT1": 1, "NT2": 1, "ST": 512, "OF": 16, "FM": 16, "UI": 1},
     B16: {"oneb": 128, "GBb": 128, "GBK": 128, "nUS": 128, "IDb": 128, "IDK": 128, "nIDb": 128, "ID2b": 128, "ID3b": 128, "nIDBb": 128, "nB02": 128,
           "it0": 128, "it1": 128, "IT2": 128, "ib": 64, "SLh": 64, "SLi": 64, "SEL": 2048, "WSA": 2048, "WSB": 2048, "FL": 512, "XG": S, "A0": S, "A1": S, "A2": S,
-          "FIT": 64, "CS": 64, "JK": 384, "INVb": 96, "KL": 576, "EA": 384, "EB": 384, "TA": 768, "GQ": 96, "PG": 96, "PN": 96, "TG": 192, "TN": 192,
-          "F1": 64, "F2": 64, "F3": 64, "SG0": 512, "SG1": 512, "SG2": 512, "N1": 512, "N2": 512},
+          "FIT": 64, "CS": 64, "JK": 384, "JL": 576, "XH": 512, "SPQ": 112, "STQ": 208, "INVb": 96, "KL": 576, "EA": 384, "EB": 384, "TA": 768, "GQ": 112, "PG": 96, "PN": 96,
+          "TG": 192, "TN": 192, "F1": 64, "F2": 64, "F3": 64, "SG0": 512, "SG1": 512, "SG2": 512, "N1": 512, "N2": 512},
     I32: {"pi": 1, "pi2": 1, "Ui": 64, "Um": 64, "UU": 64, "FQ": 64, "CA": 512, "KMi": 64, "PAR": 64, "MX": 64, "KD": 72, "XA": 6, "XI": 6, "VV": 6, "BII": 12},
-    U16: {"BQo": 6, "LO": 6, "UO": 6, "UO2": 6, "PO": 6, "TO": 12, "CDu": 6, "ROu": 6, "SQ": 6, "IXu": 64, "FX": 64},
+    U16: {"BQo": 6, "LO": 6, "UO": 6, "UO2": 6, "PO": 6, "TO": 12, "KIu": 12, "ROu": 6, "SQ": 6, "IXu": 64, "FX": 64},
 }
 _AT, SCRATCH = {}, {n: ("sbuf", [128, c], d) for n, (c, d) in _OWN.items()}
 for _d, _n in ((F32, "SF"), (B16, "SB"), (I32, "SJ"), (U16, "SU")):
@@ -210,7 +208,7 @@ def rank_program(g, core, T, topo):
     AFF(A("GB"), A("GBt"), [[16, 8], [0, 16]], O.is_ge, 15, -1)
     AFF(A("ID"), A("GB"), [[-1, 128]], O.is_equal, 0, 1)
     MS(A("WSA"), 0.0)
-    for n, c in enumerate((-4080.0, 383.0 * BIG, 255.0, 95.0)):
+    for n, c in enumerate((-4080.0, 383.0 * BIG, 255.0, -1.0, 97.0)):
         MS(A("CB", n, n + 1), c)
     TS(A("pi2"), A("pi"), 15, None, O.bitwise_and)
     TC(A("PI"), A("pi2"))
@@ -242,6 +240,7 @@ def rank_program(g, core, T, topo):
             TC(A("OFF", 256 * h, 256 * h + 256), A("C", 256 * h, 256 * h + 256))
             if h == 0 and r:
                 ACT(A("XG"), IND(A("X"), A("OFF", 0, 64)), CP)
+                ACT(A("XH"), IND(A("X"), A("OFF", 96, 128)), CP)
 
     KB3 = ("pK0", "pK1", "pN")
 
@@ -250,6 +249,8 @@ def rank_program(g, core, T, topo):
         for h in range(2):
             MM(A("pD%d" % h), A("IDb"), A("XG", 512 * h, 512 * h + 512), True, False)
             MM(A("pD%d" % h), A("IDb"), A(G, 512 * h, 512 * h + 512), False, True)
+        MM(A("pA"), A("IDb"), A("XH"), True, False)
+        MM(A("pA"), A("IDb"), A(G, 512, S), False, True)
 
         def flag(m):
             TS(A("FL", 64 * m, 64 * m + 64), A("C", 64 * m, 64 * m + 64), W - 96, 2 * m, O.is_ge, O.add)
@@ -267,9 +268,10 @@ def rank_program(g, core, T, topo):
                 TT(A("KM"), A(KB3[m % 3], 0, 64), A("KM"), O.min)
         for h in range(2):
             ACT(A("A0", 512 * h, 512 * h + 512), A("pD%d" % h), AF.Abs, bias=A("CB", 0, 1), scale=16.0)
+        ACT(A("A1", 512, S), A("pA"), AF.Abs, bias=A("CB", 0, 1), scale=16.0)
         for m in range(1, M):
             for h in range(2 if m == M - 1 else 1):
-                n = S // 2 if m == M - 1 else S
+                n = S // 2 if m in (1, M - 1) else S
                 a, b = n * h, n * h + n
                 TT(A("D%d" % (m % 2), a, b), IND(A("X"), A("OFF", 64 * m + a // 16, 64 * m + b // 16)), A(G, a, b), O.add)
                 ACT(A("A%d" % (m % 3), a, b), A("D%d" % (m % 2), a, b), AF.Abs, bias=A("CB", 0, 1), scale=16.0)
@@ -307,28 +309,31 @@ def rank_program(g, core, T, topo):
     IOTA(A("BI"), [[1, 64]], 0, 0)
     IOTA(A("i16"), [[1, 16]], 0, 0)
     IOTA(A("it0"), [[0, 8], [1, 16]], 1, 0)
-    for n, c, base in (("Q0", 96, 0), ("Q1", 96, 1), ("QT", 96, QT0), ("CDF", 96, W + 1), ("ib", 64, 0)):
+    for n, c, base in (("Q0", 96, 0), ("Q1", 96, 1), ("QT", 96, W + CAP + 1), ("ib", 64, 0)):
         IOTA(A(n), [[1, c]], base, 0)
     IOTA(A("SLh"), [[16, 64]], 0, 0)
-    IOTA(A("FW"), [[0, W + CAP]], 0, 0)
+    IOTA(A("FW"), [[0, FWW]], 0, 0)
     for n, c, base in (("KD", 72, 0), ("PW", 72, -1), ("LWn", 72, 0), ("HX", 72, 0), ("ZR", 96, 0), ("NEG", 512, -1), ("WSB", 2048, 0), ("SI0", 8, 0), ("SI1", 8, 0), ("SI2", 8, 0)):
         IOTA(A(n), [[0, c]], base, 0)
-    for n in ("G0", "G1"):
-        IOTA(A(n, S, S + CAP), [[0, CAP]], 0, 0)
+    for n, a, b in (("GQ", 96, 112), ("SPQ", 96, 112), ("STQ", 192, 208)):
+        IOTA(A(n, a, b), [[0, 16]], 0, 0)
     spread("SEL", "GB", 16)
     for n, a, c in (("IDb", "ID", 1.0), ("GBb", "GB", 1.0), ("nUS", "USf", -1.0), ("GB32", "GB", 32.0), ("GB8", "GB", 8.0), ("IDB", "ID", BIG)):
         ACT(A(n), A(a), CP, scale=c)
     ACT(A("XG"), IND(A("X"), A("OFF", 0, 64)), CP)
+    ACT(A("XH"), IND(A("X"), A("OFF", 96, 128)), CP)
     TS(A("th16"), A("thi"), 16.0, None, O.mult)
     TS(A("P512"), A("PI"), 512.0, None, O.mult)
     TS(A("P513"), A("PI"), 512.0, 1.0, O.mult, O.add)
     TS(A("P5K"), A("P513"), 10000.0, None, O.mult)
     TS(A("PL"), A("PL0"), A("P512"), None, O.add)
     TS(A("MW"), A("QM"), A("PI"), None, O.is_equal)
+    TS(A("NMW"), A("MW"), -1.0, None, O.mult)
     TS(A("RST"), A("QM"), 0.0, None, O.is_gt)
     TS(A("QB"), A("QB0"), A("PI"), 0.5, O.add, O.add)
-    TS(A("CB", 4, 5), A("PI"), 1.0 / 1024, None, O.mult)
-    TS(A("BI"), A("BI"), 1.0 / 32, A("CB", 4, 5), O.mult, O.add)
+    TS(A("QBK"), A("QB"), -97.0, None, O.add)
+    TS(A("CB", 5, 6), A("PI"), 1.0 / 1024, None, O.mult)
+    TS(A("BI"), A("BI"), 1.0 / 32, A("CB", 5, 6), O.mult, O.add)
     TS(A("I16"), A("i16"), A("PI"), None, O.is_equal)
     TS(A("LM"), A("i16"), A("PI"), BIG, O.is_le, O.mult)
     TS(A("SLi"), A("oneb", 0, 64), A("PI"), None, O.mult)
@@ -357,10 +362,12 @@ def rank_program(g, core, T, topo):
             for n, a, c in (("nB02", "B0", -2.0), ("nIDBb", "ID", -BIG), ("nIDb", "ID", -1.0), ("GBK", "GB", BIG), ("IDK", "ID", BIG),
                             ("ID2b", "ID", 2.0), ("ID3b", "ID", 3.0)):
                 ACT(A(n), A(a), CP, scale=c)
-        TS(A("F0"), A("KM"), A("th16"), None, O.is_lt)
         TC(A("KMi"), A("KM"))
+        TS(A("F0"), A("KM"), A("th16"), None, O.is_lt)
         TS(A("PAR"), A("KMi"), 1, None, O.bitwise_and)
+        TS(A("MX"), A("KMi"), 14, None, O.bitwise_and)
         TT(A("FIT"), A("F0"), A("PAR"), O.is_gt)
+        TS(A("KD", 0, 64), A("KMi"), 65520, None, O.bitwise_and)
         SCAN(A("CS"), A("one", 0, 64), A("FIT"), 0.0, O.mult, O.add)
         MM(A("pB", 0, 64), A("GBb"), A("CS"), True, True)
         MM(A("pM", 0, 64), A("GBb"), A("CS"), True, False)
@@ -368,13 +375,10 @@ def rank_program(g, core, T, topo):
         MM(A("pN", 0, 64), A("GBb"), A("CS"), True, True)
         for a in range(6):
             ACT(A("JK", 64 * a, 64 * a + 64), A("pB", 0, 64), AF.Sign, bias=A("QB", a, a + 1), scale=-1.0, acc=A("BQ", a, a + 1))
-        TS(A("MX"), A("KMi"), 14, None, O.bitwise_and)
         TT(A("LWn", 0, 64), A("MX"), A("BI"), O.add)
         TT(A("PW", 0, 64), A("pM", 0, 64), A("FIT"), O.mult)
-        TS(A("KD", 0, 64), A("KMi"), 65520, None, O.bitwise_and)
         TS(A("INVb"), A("Q0"), A("pN", 63, 64), None, O.is_ge)
         TS(A("INV"), A("INVb"), 2.0 ** -14, None, O.add)
-        ACT(A("CW", 0, 96), A("CDF"), CP)
         TS(A("BQo"), A("BQ"), 0.5, 32.0, O.mult, O.add)
         TT(A("OH"), IND(A("PW"), A("BQo")), A("Q1"), O.is_equal)
         TT(A("LG"), IND(A("LWn"), A("BQo")), A("OH"), O.mult)
@@ -382,75 +386,88 @@ def rank_program(g, core, T, topo):
         TT(A("KG"), IND(A("KD"), A("BQo")), A("OH"), O.mult)
         MM(A("pK0", 0, 96), A("GB8"), A("KG"), True, False)
         MM(A("pK0", 0, 96), A("ID"), A("Q0"), False, True)
-        TS(A("T1"), A("BQ"), 8.0, 512.0, O.mult, O.add)
+        TS(A("T1"), A("BQ"), 8.0, 608.0, O.mult, O.add)
         wrap("SL", A("pA", 0, 96), "WL")
         TC(A("LO"), A("SL", *q6))
+        TT(A("WK"), A("pK0", 0, 96), A("NMW"), O.mult)
         TT(A("CG"), IND(A("C"), A("LO")), A("OH"), O.mult)
         MM(A("pA", 0, 96), A("GB"), A("CG"), True, False)
         MM(A("pA", 0, 96), A("IDB"), A("INV"), False, True)
-        wrap("SK", A("pK0", 0, 96), "WK")
+        SCAN(A("SK"), A("RST"), A("WK"), 0.0, O.mult, O.add)
+        for a in range(6):
+            ACT(A("SGN", 96 * a, 96 * a + 96), A("pK0", 0, 96), AF.Sign, bias=A("SK", 16 * a + 15, 16 * a + 16))
         TS(A("XA"), A("SL", *q6), 32.0, None, O.mult)
-        TS(A("XI"), A("XA"), 2047, None, O.bitwise_and)
-        TT(A("T2"), A("XI"), A("T1"), O.subtract)
         wrap("SC", A("pA", 0, 96), "WC")
-        ACT(A("CR"), A("pA", 0, 96), CP)
         for a in range(6):
-            TS(A("KB", 96 * a, 96 * a + 96), A("pK0", 0, 96), A("SK", 16 * a + 15, 16 * a + 16), A("SC", 16 * a + 15, 16 * a + 16), O.is_gt, O.mult)
-        for a in range(6):
-            TT(A("KL", 96 * a, 96 * a + 96), A("KB", 96 * a, 96 * a + 96), A("pA", 0, 96), O.is_equal)
-            MM(A("pK1", 0, 96), A("GBK"), A("KL", 96 * a, 96 * a + 96), a == 0, False)
-        MM(A("pK1", 0, 96), A("IDK"), A("INVb"), False, True)
-        TC(A("SQ"), A("T2"))
-        ACT(A("GQ"), IND(A(G, 0, S), A("SQ")), CP)
-        TT(A("NCQ"), A("pK1", 0, 96), A("QT"), O.min)
-        TS(A("CUT"), A("NCQ"), 0.5, None, O.is_lt)
-        SCAN(A("RK"), A("one", 0, 96), A("CUT"), -1.0, O.mult, O.add)
-        TT(A("CD"), A("NCQ"), A("RK"), O.add)
-        wrap("SD", A("CD"), "WD")
-        TC(A("CDu"), A("SD", *q6))
-        if not last:
-            spread(("WSB", "WSA")[r], ("gwB", "gwA")[r], 1)
-        ACT(A(SI, 0, 1), A("RK", 95, 96), AF.Identity, bias=A("one", 0, 1))
-        ACT(A(SI, 7, 8), A("RK", 95, 96), AF.Identity, bias=A("CB", 3, 4), scale=-1.0)
-        SEND([A(SI)], 2 * hn, lambda: g.remote_dma_fused([to(near, en[:hn], "ai%d" % r, A(SI), A(RI)), to(far, ef[hn:], "aj%d" % r, A(SI), A(RJ))], local_sem=T.sem["loc"]))
-        TC(IND(A("CW"), A("CDu")), A("CR"))
-        wrap("SN", A("CW", 0, 96), "WN")
-        TS(A("UO"), A("SN", *q6), 15.0, W - 1.0, O.add, O.min)
+            ACT(A("KB", 96 * a, 96 * a + 96), A("SGN", 96 * a, 96 * a + 96), CP, scale=A("SC", 16 * a + 15, 16 * a + 16))
+        TS(A("UO"), A("SC", *q6), 15.0, W - 1.0, O.add, O.min)
+        TS(A("XI"), A("XA"), 2047, None, O.bitwise_and)
         TC(A("EG"), IND(A("FW"), A("UO")))
         MM(A("pM", 0, 96), A("B0"), A("EG"), True, True)
-        TS(A("PO"), A("SN", *q6), 9.0, W - 1.0, O.add, O.min)
-        ACT(A("PG"), IND(A("X"), A("PO")), CP)
-        ACT(A("PN"), A("PG"), RL, scale=-1.0)
-        MM(A("pD0", 0, 96), A("nIDb"), A("PG"), True, False)
-        MM(A("pD0", 0, 96), A("nB02"), A("PN"), False, True)
-        ACT(A(SP), A("pD0", 0, 96), RL, bias=A("CB", 2, 3))
-        SEND([A(SP)], len(en), lambda: g.remote_dma_fused([to(near, en, "ap%d" % r, A(SP), A(Z, 0, 96))], local_sem=T.sem["loc"]))
-        TT(A("VV"), A("T2"), A("SD", *q6), O.subtract)
-        TS(A("BII", 0, 6), A("VV"), 16383, 4, O.bitwise_and, O.arith_shift_right)
+        TT(A("T2"), A("XI"), A("T1"), O.subtract)
+        TS(A("PO"), A("SC", *q6), 9.0, W - 1.0, O.add, O.min)
+
+        def same(a):
+            TT(A("KL", 96 * a, 96 * a + 96), A("KB", 96 * a, 96 * a + 96), A("pA", 0, 96), O.is_equal)
+            MM(A("pK1", 0, 96), A("GBK"), A("KL", 96 * a, 96 * a + 96), a == 0, False)
+        TS(A("SQ"), A("T2"), 96.0, None, O.add)
+        TS(A("C6"), A("SC", *q6), -1.0, W - 1.0, O.add, O.min)
         wrap("S1", A("pM", 0, 96), "W1")
         TS(A("UO2"), A("S1", *q6), 6.0, W - 1.0, O.add, O.min)
         TC(A("EG2"), IND(A("FW"), A("UO2")))
         MM(A("pN", 0, 96), A("B0"), A("EG2"), True, True)
+        ACT(A("PG"), IND(A("X"), A("PO")), CP)
+        ACT(A("PN"), A("PG"), RL, scale=-1.0)
+        MM(A("pD0", 0, 96), A("nIDb"), A("PG"), True, False)
+        MM(A("pD0", 0, 96), A("nB02"), A("PN"), False, True)
+        for a in range(4):
+            same(a)
+        TT(A("W2"), A("pN", 0, 96), A("MW"), O.mult)
+        same(4)
+        SCAN(A("S2"), A("RST"), A("W2"), 0.0, O.mult, O.add)
+        same(5)
+        MM(A("pK1", 0, 96), A("IDK"), A("INVb"), False, True)
         TS(A("TO", 0, 6), A("S1", *q6), -2.0, None, O.add)
-        TS(A("BII", 6, 12), A("VV"), 15, None, O.bitwise_and)
-        TC(A("BIF"), A("BII"))
-        TS(A("ROu"), A("SN", *q6), -1.0, None, O.add)
-        wrap("S2", A("pN", 0, 96), "W2")
         TS(A("TO", 6, 12), A("S2", *q6), -2.0, None, O.add)
+        ACT(A("CR"), A("pA", 0, 96), CP)
+        ACT(A("SPQ", 0, 96), A("pD0", 0, 96), RL, bias=A("CB", 2, 3))
         ACT(A("TG"), IND(A("X"), A("TO")), CP)
         ACT(A("TN"), A("TG"), RL, scale=-1.0)
         MM(A("pD1", 0, 192), A("nIDb"), A("TG"), True, False)
         MM(A("pD1", 0, 192), A("nB02"), A("TN"), False, True)
-        ACT(A(STn), A("pD1", 0, 192), RL, bias=A("CB", 2, 3))
+        TT(A("NCQ"), A("pK1", 0, 96), A("QT"), O.min)
+        TS(A("CUT"), A("NCQ"), 0.5, None, O.is_lt)
+        SCAN(A("RK"), A("one", 0, 96), A("CUT"), -97.0, O.mult, O.add)
+        ACT(A(SI, 0, 1), A("RK", 95, 96), AF.Identity, bias=A("CB", 4, 5))
+        ACT(A(SI, 7, 8), A("RK", 95, 96), AF.Identity, bias=A("CB", 3, 4), scale=-1.0)
+        SEND([A(SI)], 2 * hn, lambda: g.remote_dma_fused([to(near, en[:hn], "ai%d" % r, A(SI), A(RI)), to(far, ef[hn:], "aj%d" % r, A(SI), A(RJ))], local_sem=T.sem["loc"]))
+        for a in range(6):
+            ACT(A("JL", 96 * a, 96 * a + 96), A("RK"), AF.Sign, bias=A("QBK", a, a + 1), scale=-1.0, acc=A("BK", a, a + 1))
+        ACT(A("STQ", 0, 192), A("pD1", 0, 192), RL, bias=A("CB", 2, 3))
+        TT(A("CD"), A("NCQ"), A("RK"), O.add)
+        TT(A("LEN"), A("pN", 0, 96), A("CR"), O.subtract)
+        TT(A("WD"), A("CD"), A("MW"), O.mult)
+        TS(A("KIu", 0, 6), A("BK"), 0.5, 48.0, O.mult, O.add)
+        TS(A("KIu", 6, 12), A("BK"), 0.5, 144.0, O.mult, O.add)
+        ACT(A(SP), IND(A("SPQ"), A("KIu", 0, 6)), CP)
+        SEND([A(SP)], len(en), lambda: g.remote_dma_fused([to(near, en, "ap%d" % r, A(SP), A(Z, 0, 96))], local_sem=T.sem["loc"]))
+        ACT(A(STn), IND(A("STQ"), A("KIu")), CP)
         SEND([A(STn)], len(ef), lambda: g.remote_dma_fused([to(far, ef, "at%d" % r, A(STn), A(Z, 96, 288))], local_sem=T.sem["loc"]))
+        ACT(A("GQ", 0, 96), IND(A(G, 0, S), A("SQ")), CP)
+        ACT(A(G, S, S + CAP), IND(A("GQ"), A("KIu", 0, 6)), CP)
+        SCAN(A("SD"), A("RST"), A("WD"), 0.0, O.mult, O.add)
+        TT(A("R6"), A("C6"), A("SD", *q6), O.max)
+        TT(A("VV"), A("T2"), A("SD", *q6), O.subtract)
+        TC(A("ROu"), A("R6"))
+        TS(A("BII", 0, 6), A("VV"), 16383, 4, O.bitwise_and, O.arith_shift_right)
+        TS(A("BII", 6, 12), A("VV"), 15, None, O.bitwise_and)
         LAND(A(RI), "ai%d" % r, hn)
         LAND(A(RJ), "aj%d" % r, len(ef) - hn)
         LAND(A(Z, 0, 96), "ap%d" % r, len(en))
         LAND(A(Z, 96, 288), "at%d" % r, len(ef))
-        TT(A("LEN"), A("pN", 0, 96), A("CW", 0, 96), O.subtract)
         TC(IND(A("FW"), A("ROu")), A("LEN"))
         DMA("y", A("LW"), A("FW", 0, W, rows=slice(1, 128, 16)))
-        TC(IND(A(G, S, GW), A("CDu")), A("GQ"))
+        TC(A("BIF"), A("BII"))
         for a in range(6):
             ACT(A("EA", 64 * a, 64 * a + 64), A("ib"), AF.Abs, bias=A("BIF", a, a + 1), scale=-1.0)
         ACT(A("EB"), A("EA"), RL, bias=A("one", 0, 1), scale=-1.0)
@@ -462,7 +479,7 @@ def rank_program(g, core, T, topo):
         MM(A("pA", 0, 64), A("IDb"), A("SLi"), False, False)
         for a in range(6):
             MM(A("pA", 0, 64), A("TA", 128 * a, 128 * a + 128), A("EB", 64 * a, 64 * a + 64), False, a == 5)
-        ACT(A("M1"), A("CW", 0, 96), RL, bias=A("P5K"), scale=-10000.0)
+        ACT(A("M1"), A("CR"), RL, bias=A("P5K"), scale=-10000.0)
         TT(A("M2"), A("pN", 0, 96), A("M1"), O.min)
         RED(A("RD"), A("M2"), O.max)
         TS(A("IN"), A("RD"), A("P512"), 0.0, O.subtract, O.max)
@@ -475,12 +492,11 @@ def rank_program(g, core, T, topo):
         if not last:
             MM(A("pK0"), A("IDb"), A("X0"), True, False)
             MM(A("pK0"), A("nIDBb"), A(SG), False, True)
-            ACT(A("X0"), A("pK0"), CP)
-            DMA("y", A("X", 0, W, rows=slice(0, 128, 16)), A("X0"))
+            spread(("WSB", "WSA")[r], ("gwB", "gwA")[r], 1)
             TC(IND(A("FW"), A("ROu")), A("ZR"))
-        ACT(A("NT1"), A(RI, 0, 1), AF.Identity, bias=A(RJ, 0, 1))
-        ACT(A("NT2"), A("NT1"), AF.Identity, bias=A(RJ, 0, 1))
+        TT(A("NT1"), A(RI, 0, 1), A(RJ, 0, 1), O.add)
         TS(A("F1"), A("SLf"), A(RI, 0, 1), A(RI, 7, 8), O.is_ge, O.mult)
+        TT(A("NT2"), A("NT1"), A(RJ, 0, 1), O.add)
         TS(A("F2"), A("SLf"), A("NT1"), A(RJ, 7, 8), O.is_ge, O.mult)
         TS(A("F3"), A("SLf"), A("NT2"), A(RJ, 7, 8), O.is_ge, O.mult)
         for k, n in enumerate(("SLh", "SLi", "F1", "F2", "F3")):
@@ -490,6 +506,9 @@ def rank_program(g, core, T, topo):
         ACT(A(H, S // 2, S), IND(A(Z), A("FX", 32, 64)), CP)
         if last:
             DMA("y", XT(T.yg[:, :]), A(H, 0, S))
+        else:
+            TC(A("X0"), A("pK0"))
+            DMA("y", A("X", 0, W, rows=slice(0, 128, 16)), A("X0"))
         if r:
             MM(A("pK1"), A("IDb"), A(SG), True, False)
             MM(A("pK1"), A("nIDb"), A("SG0"), False, r == 1)

@@ -9,7 +9,7 @@ F32, B16, I32, U16 = "float32", "bfloat16", "int32", "uint16"
 _OWN = {
     "X": (W, B16), "FW": (FWW, F32), "G0": (S + CAP, B16), "G1": (S + CAP, B16), "X0": (512, B16),
     "wti": (3, I32), "kmi": (8, I32), "thi": (1, I32), "LW": (512, F32), "U2": (512, F32), "YC": (512, F32),
-    "UL": (512, F32), "NO": (512, F32), "PL": (512, F32), "D0": (S, F32), "D1": (S, F32), "C": (512, I32), "OFF": (512, U16),
+    "UL": (512, F32), "NO": (512, F32), "PL": (512, F32), "D0": (S, F32), "D1": (S, F32), "D2": (S, F32), "C": (512, I32), "OFF": (512, U16),
 }
 for _r in range(RO):
     _OWN.update({"SI%d" % _r: (8, F32), "SP%d" % _r: (96, B16), "ST%d" % _r: (192, B16), "RI%d" % _r: (8, F32), "RJ%d" % _r: (8, F32), "Z%d" % _r: (288 + S, B16)})
@@ -21,7 +21,7 @@ _PART = {
           "W2": 96, "S2": 96, "KB": 576, "SGN": 576, "C6": 6, "R6": 6, "CR": 96, "CUT": 96, "NCQ": 96, "RK": 96, "CD": 96, "WD": 96, "SD": 96, "LEN": 96, "ZR": 96,
           "M1": 96, "M2": 96, "RD": 1, "IN": 1, "T1": 6, "T2": 6, "BIF": 12, "HX": 72, "IX": 64, "SLf": 64, "NT1": 1, "NT2": 1, "ST": 512, "OF": 16, "FM": 16, "UI": 1},
     B16: {"oneb": 128, "GBb": 128, "GBK": 128, "nUS": 128, "IDb": 128, "IDK": 128, "nIDb": 128, "ID2b": 128, "ID3b": 128, "nIDBb": 128, "nB02": 128,
-          "it0": 128, "it1": 128, "IT2": 128, "ib": 64, "SLh": 64, "SLi": 64, "SEL": 2048, "WSA": 2048, "WSB": 2048, "FL": 512, "XG": S, "A0": S, "A1": S, "A2": S,
+          "it0": 128, "it1": 128, "IT2": 128, "ib": 64, "SLh": 64, "SLi": 64, "SEL": 2048, "WSA": 2048, "WSB": 2048, "FL": 512, "M2C": 512, "XG": S, "A0": S, "A1": S, "A2": S,
           "FIT": 64, "CS": 64, "JK": 384, "JL": 576, "XH": 512, "SPQ": 112, "STQ": 208, "INVb": 96, "KL": 576, "EA": 384, "EB": 384, "TA": 768, "GQ": 112, "PG": 96, "PN": 96,
           "TG": 192, "TN": 192, "F1": 64, "F2": 64, "F3": 64, "SG0": 512, "SG1": 512, "SG2": 512, "N1": 512, "N2": 512},
     I32: {"pi": 1, "pi2": 1, "Ui": 64, "Um": 64, "UU": 64, "FQ": 64, "CA": 512, "KMi": 64, "PAR": 64, "MX": 64, "KD": 72, "XA": 6, "XI": 6, "VV": 6, "BII": 12},
@@ -242,7 +242,7 @@ def rank_program(g, core, T, topo):
                 ACT(A("XG"), IND(A("X"), A("OFF", 0, 64)), CP)
                 ACT(A("XH"), IND(A("X"), A("OFF", 96, 128)), CP)
 
-    KB3 = ("pK0", "pK1", "pN")
+    KB4 = ("pK0", "pK1", "pN", "pM")
 
     def scores(r):
         G = "G%d" % (r % 2)
@@ -252,20 +252,22 @@ def rank_program(g, core, T, topo):
         MM(A("pA"), A("IDb"), A("XH"), True, False)
         MM(A("pA"), A("IDb"), A(G, 512, S), False, True)
 
-        def flag(m):
-            TS(A("FL", 64 * m, 64 * m + 64), A("C", 64 * m, 64 * m + 64), W - 96, 2 * m, O.is_ge, O.add)
+        def flag(h):
+            TS(A("FL", 256 * h, 256 * h + 256), A("C", 256 * h, 256 * h + 256), W - 96, None, O.is_ge)
 
         def keys(m):
-            k = KB3[m % 3]
+            k = KB4[m % 4]
             for i in range(16):
                 MM(A(k, 0, 64), A("SEL", 128 * i, 128 * i + 128), A("A%d" % (m % 3), i, S, 16), i == 0, False)
-            MM(A(k, 0, 64), A("IDb"), A("FL", 64 * m, 64 * m + 64), False, True)
+            MM(A(k, 0, 64), A("IDb"), A("FL", 64 * m, 64 * m + 64), False, m == 0)
+            if m:
+                MM(A(k, 0, 64), A("IDb"), A("M2C", 64 * m, 64 * m + 64), False, True)
 
         def least(m):
             if m == 0:
-                TC(A("KM"), A(KB3[0], 0, 64))
+                TC(A("KM"), A(KB4[0], 0, 64))
             elif m > 0:
-                TT(A("KM"), A(KB3[m % 3], 0, 64), A("KM"), O.min)
+                TT(A("KM"), A(KB4[m % 4], 0, 64), A("KM"), O.min)
         for h in range(2):
             ACT(A("A0", 512 * h, 512 * h + 512), A("pD%d" % h), AF.Abs, bias=A("CB", 0, 1), scale=16.0)
         ACT(A("A1", 512, S), A("pA"), AF.Abs, bias=A("CB", 0, 1), scale=16.0)
@@ -273,32 +275,40 @@ def rank_program(g, core, T, topo):
             for h in range(2 if m == M - 1 else 1):
                 n = S // 2 if m in (1, M - 1) else S
                 a, b = n * h, n * h + n
-                TT(A("D%d" % (m % 2), a, b), IND(A("X"), A("OFF", 64 * m + a // 16, 64 * m + b // 16)), A(G, a, b), O.add)
-                ACT(A("A%d" % (m % 3), a, b), A("D%d" % (m % 2), a, b), AF.Abs, bias=A("CB", 0, 1), scale=16.0)
-            if m == 3:
+                TT(A("D%d" % (m % 3), a, b), IND(A("X"), A("OFF", 64 * m + a // 16, 64 * m + b // 16)), A(G, a, b), O.add)
+                ACT(A("A%d" % (m % 3), a, b), A("D%d" % (m % 3), a, b), AF.Abs, bias=A("CB", 0, 1), scale=16.0)
+            if m == 5 and r == 0:
                 ACT(A("NO"), A("X0"), RL, bias=A("CB", 1, 2), scale=-2 * BIG)
             if m == 1:
                 flag(0)
                 keys(0)
-            flag(m)
+            if m == 3:
+                flag(1)
             keys(m)
-            least(m - 2)
+            least(m - 3)
+        least(M - 3)
         least(M - 2)
-        utable()
+        utable(0)
+        if r:
+            TC(IND(A("FW"), A("ROu")), A("ZR"))
         least(M - 1)
 
     def wrap(dst, src, tmp):
         TT(A(tmp), src, A("MW"), O.mult)
         SCAN(A(dst), A("RST"), A(tmp), 0.0, O.mult, O.add)
 
-    def utable():
-        SCAN(A("UL", s=-1), A("NO", s=-1), A("PL", s=-1), float(W + 1), O.min, O.max)
-        TS(A("OF"), A("I16"), A("UL", 0, 1), None, O.mult)
-        MM(A("pD0", 0, 16), A("GB"), A("OF"), True, True)
-        TT(A("FM"), A("pD0", 0, 16), A("LM"), O.max)
-        RED(A("UI"), A("FM"), O.min)
-        TS(A("U2"), A("UL"), A("UI"), None, O.min)
-        DMA("y", A("FW", 0, W, rows=slice(0, 128, 16)), A("U2"))
+    def utable(k):
+        if k == 0:
+            SCAN(A("UL", s=-1), A("NO", s=-1), A("PL", s=-1), float(W + 1), O.min, O.max)
+            TS(A("OF"), A("I16"), A("UL", 0, 1), None, O.mult)
+            MM(A("pD0", 0, 16), A("GB"), A("OF"), True, True)
+        elif k == 1:
+            TT(A("FM"), A("pD0", 0, 16), A("LM"), O.max)
+        elif k == 2:
+            RED(A("UI"), A("FM"), O.min)
+        else:
+            TS(A("U2"), A("UL"), A("UI"), None, O.min)
+            DMA("y", A("FW", 0, W, rows=slice(0, 128, 16)), A("U2"))
 
     lists(0)
     IOTA(A("QM"), [[0, 6], [1, 16]], 0, 0)
@@ -312,6 +322,7 @@ def rank_program(g, core, T, topo):
     for n, c, base in (("Q0", 96, 0), ("Q1", 96, 1), ("QT", 96, W + CAP + 1), ("ib", 64, 0)):
         IOTA(A(n), [[1, c]], base, 0)
     IOTA(A("SLh"), [[16, 64]], 0, 0)
+    IOTA(A("M2C"), [[2, 8], [0, 64]], 0, 0)
     IOTA(A("FW"), [[0, FWW]], 0, 0)
     for n, c, base in (("KD", 72, 0), ("PW", 72, -1), ("LWn", 72, 0), ("HX", 72, 0), ("ZR", 96, 0), ("NEG", 512, -1), ("WSB", 2048, 0), ("SI0", 8, 0), ("SI1", 8, 0), ("SI2", 8, 0)):
         IOTA(A(n), [[0, c]], base, 0)
@@ -364,9 +375,11 @@ def rank_program(g, core, T, topo):
                 ACT(A(n), A(a), CP, scale=c)
         TC(A("KMi"), A("KM"))
         TS(A("F0"), A("KM"), A("th16"), None, O.is_lt)
+        utable(1)
         TS(A("PAR"), A("KMi"), 1, None, O.bitwise_and)
         TS(A("MX"), A("KMi"), 14, None, O.bitwise_and)
         TT(A("FIT"), A("F0"), A("PAR"), O.is_gt)
+        utable(2)
         TS(A("KD", 0, 64), A("KMi"), 65520, None, O.bitwise_and)
         SCAN(A("CS"), A("one", 0, 64), A("FIT"), 0.0, O.mult, O.add)
         MM(A("pB", 0, 64), A("GBb"), A("CS"), True, True)
@@ -375,6 +388,13 @@ def rank_program(g, core, T, topo):
         MM(A("pN", 0, 64), A("GBb"), A("CS"), True, True)
         for a in range(6):
             ACT(A("JK", 64 * a, 64 * a + 64), A("pB", 0, 64), AF.Sign, bias=A("QB", a, a + 1), scale=-1.0, acc=A("BQ", a, a + 1))
+        if last:
+            MM(A("pK1"), A("IDb"), A("SG1"), True, False)
+            MM(A("pK1"), A("nIDb"), A("SG0"), False, True)
+            ACT(A("N1"), A("pK1"), RL)
+        if not last:
+            spread(("WSB", "WSA")[r], ("gwB", "gwA")[r], 1)
+        utable(3)
         TT(A("LWn", 0, 64), A("MX"), A("BI"), O.add)
         TT(A("PW", 0, 64), A("pM", 0, 64), A("FIT"), O.mult)
         TS(A("INVb"), A("Q0"), A("pN", 63, 64), None, O.is_ge)
@@ -430,6 +450,7 @@ def rank_program(g, core, T, topo):
         TS(A("TO", 0, 6), A("S1", *q6), -2.0, None, O.add)
         TS(A("TO", 6, 12), A("S2", *q6), -2.0, None, O.add)
         ACT(A("CR"), A("pA", 0, 96), CP)
+        ACT(A("M1"), A("CR"), RL, bias=A("P5K"), scale=-10000.0)
         ACT(A("SPQ", 0, 96), A("pD0", 0, 96), RL, bias=A("CB", 2, 3))
         ACT(A("TG"), IND(A("X"), A("TO")), CP)
         ACT(A("TN"), A("TG"), RL, scale=-1.0)
@@ -447,6 +468,9 @@ def rank_program(g, core, T, topo):
         TT(A("CD"), A("NCQ"), A("RK"), O.add)
         TT(A("LEN"), A("pN", 0, 96), A("CR"), O.subtract)
         TT(A("WD"), A("CD"), A("MW"), O.mult)
+        SCAN(A("SD"), A("RST"), A("WD"), 0.0, O.mult, O.add)
+        TT(A("R6"), A("C6"), A("SD", *q6), O.max)
+        TT(A("VV"), A("T2"), A("SD", *q6), O.subtract)
         TS(A("KIu", 0, 6), A("BK"), 0.5, 48.0, O.mult, O.add)
         TS(A("KIu", 6, 12), A("BK"), 0.5, 144.0, O.mult, O.add)
         ACT(A(SP), IND(A("SPQ"), A("KIu", 0, 6)), CP)
@@ -455,9 +479,6 @@ def rank_program(g, core, T, topo):
         SEND([A(STn)], len(ef), lambda: g.remote_dma_fused([to(far, ef, "at%d" % r, A(STn), A(Z, 96, 288))], local_sem=T.sem["loc"]))
         ACT(A("GQ", 0, 96), IND(A(G, 0, S), A("SQ")), CP)
         ACT(A(G, S, S + CAP), IND(A("GQ"), A("KIu", 0, 6)), CP)
-        SCAN(A("SD"), A("RST"), A("WD"), 0.0, O.mult, O.add)
-        TT(A("R6"), A("C6"), A("SD", *q6), O.max)
-        TT(A("VV"), A("T2"), A("SD", *q6), O.subtract)
         TC(A("ROu"), A("R6"))
         TS(A("BII", 0, 6), A("VV"), 16383, 4, O.bitwise_and, O.arith_shift_right)
         TS(A("BII", 6, 12), A("VV"), 15, None, O.bitwise_and)
@@ -473,34 +494,33 @@ def rank_program(g, core, T, topo):
         ACT(A("EB"), A("EA"), RL, bias=A("one", 0, 1), scale=-1.0)
         for a in range(6):
             TS(A("TA", 128 * a, 128 * a + 128), A("IT2"), A("BIF", 6 + a, 7 + a), None, O.is_ge)
+            if a == 1:
+                TT(A("M2"), A("pN", 0, 96), A("M1"), O.min)
+            if a == 3:
+                RED(A("RD"), A("M2"), O.max)
+        TS(A("IN"), A("RD"), A("P512"), 0.0, O.subtract, O.max)
         for a in range(6):
             MM(A("pB", 0, 64), A("GBb"), A("EB", 64 * a, 64 * a + 64), a == 0, a == 5)
         MM(A("pA", 0, 64), A("IDb"), A("SLh"), True, False)
         MM(A("pA", 0, 64), A("IDb"), A("SLi"), False, False)
         for a in range(6):
             MM(A("pA", 0, 64), A("TA", 128 * a, 128 * a + 128), A("EB", 64 * a, 64 * a + 64), False, a == 5)
-        ACT(A("M1"), A("CR"), RL, bias=A("P5K"), scale=-10000.0)
-        TT(A("M2"), A("pN", 0, 96), A("M1"), O.min)
-        RED(A("RD"), A("M2"), O.max)
-        TS(A("IN"), A("RD"), A("P512"), 0.0, O.subtract, O.max)
         SCAN(A("HX", 1, 65), A("one", 0, 64), A("pB", 0, 64), 0.0, O.mult, O.add)
         TT(A("IX"), A("pA", 0, 64), A("HX", 0, 64), O.add)
         TC(A("IXu"), A("IX"))
         ACT(A(Z, 288, 288 + S), IND(A(G, 0, S + CAP), A("IXu")), CP)
-        SCAN(A("ST"), A("NEG"), A("LW"), A("IN"), O.add, O.max)
-        ACT(A(SG), A("ST"), AF.Sign)
-        if not last:
-            MM(A("pK0"), A("IDb"), A("X0"), True, False)
-            MM(A("pK0"), A("nIDBb"), A(SG), False, True)
-            spread(("WSB", "WSA")[r], ("gwB", "gwA")[r], 1)
-            TC(IND(A("FW"), A("ROu")), A("ZR"))
         TT(A("NT1"), A(RI, 0, 1), A(RJ, 0, 1), O.add)
         TS(A("F1"), A("SLf"), A(RI, 0, 1), A(RI, 7, 8), O.is_ge, O.mult)
         TT(A("NT2"), A("NT1"), A(RJ, 0, 1), O.add)
         TS(A("F2"), A("SLf"), A("NT1"), A(RJ, 7, 8), O.is_ge, O.mult)
         TS(A("F3"), A("SLf"), A("NT2"), A(RJ, 7, 8), O.is_ge, O.mult)
+        SCAN(A("ST"), A("NEG"), A("LW"), A("IN"), O.add, O.max)
+        ACT(A(SG), A("ST"), AF.Sign)
         for k, n in enumerate(("SLh", "SLi", "F1", "F2", "F3")):
             MM(A("pM", 0, 64), A("IDb"), A(n), k == 0, k == 4)
+        if not last:
+            MM(A("pK0"), A("IDb"), A("X0"), True, False)
+            MM(A("pK0"), A("nIDBb"), A(SG), False, True)
         TC(A("FX"), A("pM", 0, 64))
         TC(A(H, 0, S // 2), IND(A(Z), A("FX", 0, 32)))
         ACT(A(H, S // 2, S), IND(A(Z), A("FX", 32, 64)), CP)
@@ -508,14 +528,13 @@ def rank_program(g, core, T, topo):
             DMA("y", XT(T.yg[:, :]), A(H, 0, S))
         else:
             TC(A("X0"), A("pK0"))
+            ACT(A("NO"), A("X0"), RL, bias=A("CB", 1, 2), scale=-2 * BIG)
             DMA("y", A("X", 0, W, rows=slice(0, 128, 16)), A("X0"))
-        if r:
-            MM(A("pK1"), A("IDb"), A(SG), True, False)
-            MM(A("pK1"), A("nIDb"), A("SG0"), False, r == 1)
-            if r == 2:
-                MM(A("pK1"), A("nIDb"), A("N1"), False, True)
-            ACT(A("N%d" % r), A("pK1"), RL)
         if last:
+            MM(A("pK1"), A("IDb"), A(SG), True, False)
+            MM(A("pK1"), A("nIDb"), A("SG0"), False, False)
+            MM(A("pK1"), A("nIDb"), A("N1"), False, True)
+            ACT(A("N2"), A("pK1"), RL)
             MM(A("pD0"), A("IDb"), A("SG0"), True, False)
             MM(A("pD0"), A("ID2b"), A("N1"), False, False)
             MM(A("pD0"), A("ID3b"), A("N2"), False, True)

from concourse.bass import DstId, RemoteDMATransfer
from concourse.mybir import AluOpType as O, ActivationFunctionType as AF, AxisListType

W, S, M, CAP, RO = 8192, 1024, 8, 96, 3
BIG = 16384.0
FWW = W + 2 * CAP

F32, B16, I32, U16 = "float32", "bfloat16", "int32", "uint16"
_OWN = {
    "X": (W, B16), "FW": (FWW, F32), "G0": (S + CAP, B16), "G1": (S + CAP, B16), "X0": (512, B16),
    "wti": (3, I32), "kmi": (8, I32), "thi": (1, I32), "LW": (512, F32), "U2": (512, F32), "YC": (512, F32),
    "UL": (512, F32), "NO": (512, F32), "PL": (512, F32), "D0": (S, F32), "D1": (S, F32), "D2": (S, F32), "C": (512, I32), "OFF": (512, U16),
}
for _r in range(RO):
    _OWN.update({"SI%d" % _r: (8, F32), "SP%d" % _r: (96, B16), "ST%d" % _r: (192, B16), "RI%d" % _r: (8, F32), "RJ%d" % _r: (8, F32), "Z%d" % _r: (288 + S, B16)})
_PART = {
    F32: {"wtf": 3, "kmf": 8, "th16": 1, "one": 128, "GB": 128, "GBt": 128, "GB8": 128, "GB32": 128, "B0": 128, "ID": 128, "IDB": 128, "USf": 128,
          "PI": 1, "P512": 1, "P513": 1, "P5K": 1, "CB": 16, "QM": 96, "MW": 96, "RST": 96, "Q0": 96, "Q1": 96, "QT": 96, "NMW": 96, "BI": 64, "QB0": 6, "QB": 6, "QBK": 6, "BK": 6,
          "i16": 16, "I16": 16, "LM": 16, "PL0": 512, "NEG": 512, "gwA": 8, "gwB": 8, "Uf": 64, "KM": 64, "F0": 64, "PW": 72, "LWn": 72, "BQ": 6, "OH": 96,
          "LG": 96, "KG": 96, "WL": 96, "SL": 96, "INV": 96, "CG": 96, "WK": 96, "SK": 96, "WC": 96, "SC": 96, "EG": 96, "EG2": 96, "W1": 96, "S1": 96,
          "W2": 96, "S2": 96, "KB": 576, "SGN": 576, "C6": 6, "R6": 6, "CR": 96, "CUT": 96, "NCQ": 96, "RK": 96, "CD": 96, "WD": 96, "SD": 96, "LEN": 96, "ZR": 96,
          "M1": 96, "M2": 96, "RD": 1, "IN": 1, "T1": 6, "T2": 6, "BIF": 12, "HX": 72, "IX": 64, "SLf": 64, "NT1": 1, "NT2": 1, "ST": 512, "OF": 16, "FM": 16, "UI": 1},
    B16: {"oneb": 128, "GBb": 128, "GBK": 128, "nUS": 128, "IDb": 128, "IDK": 128, "nIDb": 128, "ID2b": 128, "ID3b": 128, "nIDBb": 128, "nB02": 128,
          "it0": 128, "it1": 128, "IT2": 128, "ib": 64, "SLh": 64, "SLi": 64, "SEL": 2048, "WSA": 2048, "WSB": 2048, "FL": 512, "M2C": 512, "XG": S, "A0": S, "A1": S, "A2": S,
          "FIT": 64, "CS": 64, "JK": 384, "JL": 576, "XH": 512, "SPQ": 112, "STQ": 208, "INVb": 96, "KL": 576, "EA": 384, "EB": 384, "TA": 768, "GQ": 112, "PG": 96, "PN": 96,
          "TG": 192, "TN": 192, "F1": 64, "F2": 64, "F3": 64, "SG0": 512, "SG1": 512, "SG2": 512, "N1": 512, "N2": 512},
    I32: {"pi": 1, "pi2": 1, "Ui": 64, "Um": 64, "UU": 64, "FQ": 64, "CA": 512, "KMi": 64, "PAR": 64, "MX": 64, "KD": 72, "XA": 6, "XI": 6, "VV": 6, "BII": 12},
    U16: {"BQo": 6, "LO": 6, "UO": 6, "UO2": 6, "PO": 6, "TO": 12, "KIu": 12, "ROu": 6, "SQ": 6, "IXu": 64, "FX": 64},
}
_AT, SCRATCH = {}, {n: ("sbuf", [128, c], d) for n, (c, d) in _OWN.items()}
for _d, _n in ((F32, "SF"), (B16, "SB"), (I32, "SJ"), (U16, "SU")):
    _c = 0
    for _k, _w in _PART[_d].items():
        _AT[_k] = (_n, _c, _w)
        _c += -(-_w // 16) * 16
    SCRATCH[_n] = ("sbuf", [128, _c], _d)
_PS = ["pA", "pB", "pM", "pN", "pK0", "pK1", "pD0", "pD1"]
SCRATCH.update({n: ("psum", [128, 512], F32) for n in _PS})
SEMAPHORES = ["sv", "ss", "st", "sg", "loc"] + ["a%s%d" % (k, r) for k in "ijpt" for r in range(RO)] + ["d%d" % k for k in range(30)]


def _queues(g, T):
    Q = {"v": g.vector, "s": g.scalar, "t": g.tensor, "g": g, "y": g.sync}
    ENG = {"v": "sv", "s": "ss", "t": "st", "g": "sg"}
    cnt, seen, acc, no = {}, {q: {} for q in Q}, {}, [0, 0]

    def A(n, a=0, b=None, s=1, rows=None):
        m, off, w = _AT[n] if n in _AT else (n, 0, T[n].shape[1])
        b = w if b is None else b
        a, b, t = a + off, b + off, T[m]
        if rows is not None:
            ap = t[rows, a:b]
        elif s < 0:
            ap = t[:, ::-1]
        elif s > 1:
            ap = t[:, a:b:s]
        else:
            ap = t[:, a:b]
        return (ap, ((m, a, b, abs(s)),), ())

    def X(ap):
        return (ap, (), ())

    def IND(win, off):
        return (win[0].indirect(off[0]), win[1], off[1])

    def need(q, outs, ins, chain=False):
        deps = []
        for w, regs in ((True, outs), (False, ins)):
            for (n, a, b, s) in regs:
                ps = n in _PS
                for rec in acc.get(n, ()):
                    rw, rq, sem, val, ra, rb, rs, clk, k = rec
                    if not (w or rw or (ps and rq != q)):
                        continue
                    if not (ps and rq != q):
                        if b <= ra or rb <= a or (s == rs and s > 1 and (a - ra) % s):
                            continue
                        if rq == q and chain and w:
                            continue
                    deps.append((k, sem, val, clk))
        deps.sort(key=lambda d: -d[0])
        for k, sem, val, clk in deps:
            if seen[q].get(sem, 0) >= val:
                continue
            Q[q].wait_ge(T.sem[sem], val)
            for s2, v2 in clk.items():
                if seen[q].get(s2, 0) < v2:
                    seen[q][s2] = v2
            seen[q][sem] = max(val, seen[q].get(sem, 0))

    def note(q, sem, val, clk, outs, ins):
        no[0] += 1
        for w, regs in ((True, outs), (False, ins)):
            for (n, a, b, s) in regs:
                old = acc.get(n, [])
                if w and s == 1:
                    old = [x for x in old if not (a <= x[4] and x[5] <= b)]
                old.append((w, q, sem, val, a, b, s, clk, no[0]))
                acc[n] = old

    def split(outs, ins):
        o = [x for p in outs for x in p[1]]
        i = [x for p in outs for x in p[2]] + [x for p in ins if isinstance(p, tuple) for x in p[1] + p[2]]
        return o, i

    def run(q, outs, ins, call, chain=False):
        o, i = split(outs, ins)
        need(q, o, i, chain)
        sem = ENG[q]
        cnt[sem] = cnt.get(sem, 0) + 1
        call().then_inc(T.sem[sem], 1)
        clk = dict(seen[q])
        clk[sem] = cnt[sem]
        note(q, sem, cnt[sem], clk, o, i)

    def v(x):
        return x[0] if isinstance(x, tuple) else x

    V, SC, TE = g.vector, g.scalar, g.tensor

    def TT(o, a, b, op):
        run("v", [o], [a, b], lambda: V.tensor_tensor(out=o[0], in0=a[0], in1=b[0], op=op))

    def TS(o, a, s1, s2, op0, op1=None):
        if op1 is None:
            run("v", [o], [a, s1], lambda: V.tensor_scalar(out=o[0], in0=a[0], scalar1=v(s1), scalar2=None, op0=op0))
        else:
            run("v", [o], [a, s1, s2], lambda: V.tensor_scalar(out=o[0], in0=a[0], scalar1=v(s1), scalar2=v(s2), op0=op0, op1=op1))

    def TC(o, a):
        run("v", [o], [a], lambda: V.tensor_copy(out=o[0], in_=a[0]))

    def MS(o, c):
        run("v", [o], [], lambda: V.memset(o[0], c))

    def RED(o, a, op):
        run("v", [o], [a], lambda: V.tensor_reduce(out=o[0], in_=a[0], axis=AxisListType.X, op=op))

    def SCAN(o, a, b, init, op0, op1):
        run("v", [o], [a, b, init], lambda: V.tensor_tensor_scan(out=o[0], data0=a[0], data1=b[0], initial=v(init), op0=op0, op1=op1))

    def ACT(o, a, f, bias=0.0, scale=1.0, acc=None):
        if acc is None:
            run("s", [o], [a, bias, scale], lambda: SC.activation(out=o[0], in_=a[0], func=f, bias=v(bias), scale=v(scale)))
        else:
            run("s", [o, acc], [a, bias, scale], lambda: SC.activation(out=o[0], in_=a[0], func=f, bias=v(bias), scale=v(scale), accum_out=acc[0]))

    def MM(o, l, r, start, stop):
        run("t", [o], [l, r], lambda: TE.matmul(o[0], l[0], r[0], start=start, stop=stop), not start)

    def IOTA(o, pat, base, cm):
        run("g", [o], [], lambda: g.iota(o[0], pat, base, cm, allow_small_or_imprecise_dtypes=True))

    def AFF(o, a, pat, op, base, cm):
        run("g", [o], [a], lambda: g.affine_select(o[0], a[0], pat, op, 0.0, base, cm))

    def DMA(q, o, a):
        os_, is_ = split([o], [a])
        need(q, os_, is_)
        sem = "d%d" % no[1]
        no[1] += 1
        Q[q].dma_start(o[0], a[0]).then_inc(T.sem[sem], 16)
        cnt[sem] = 16
        clk = dict(seen[q])
        clk[sem] = 16
        note("dma", sem, 16, clk, os_, is_)

    def SEND(srcs, engines, call):
        o, i = split([], srcs)
        need("g", o, i)
        call()
        cnt["loc"] = cnt.get("loc", 0) + engines
        note("rem", "loc", cnt["loc"], {}, o, i)

    def LAND(dst, sem, val):
        cnt[sem] = val
        note("rem", sem, val, {sem: val}, list(dst[1]), [])

    def END():
        for sem in cnt:
            if max(seen[q].get(sem, 0) for q in Q) < cnt[sem]:
                g.wait_ge(T.sem[sem], cnt[sem])

    return A, X, IND, TT, TS, TC, MS, RED, SCAN, ACT, MM, IOTA, AFF, DMA, SEND, LAND, END


def rank_program(g, core, T, topo):
    rank = T.rank_of(core)
    if rank is None:
        return
    A, XT, IND, TT, TS, TC, MS, RED, SCAN, ACT, MM, IOTA, AFF, DMA, SEND, LAND, END = _queues(g, T)
    CP, RL = AF.Copy, AF.Relu
    q6 = (15, 96, 16)

    DMA("y", A("G0", 0, S), XT(T.gd[:, :]))
    DMA("s", A("wti"), XT(T.wt[:, :]))
    DMA("s", A("kmi"), XT(T.km[:, :]))
    DMA("s", A("thi"), XT(T.th[:, :]))
    DMA("s", A("X", W // 2, W), XT(T.xs[:, W // 2:W]))
    DMA("y", A("X", 0, W // 2), XT(T.xs[:, 0:W // 2]))
    DMA("y", A("X0"), XT(T.xs[0::16, :]))

    MS(A("one"), 1.0)
    MS(A("oneb"), 1.0)
    IOTA(A("pi"), [[0, 1]], 0, 1)
    AFF(A("GBt"), A("one"), [[-16, 8], [0, 16]], O.is_ge, 0, 1)
    AFF(A("GB"), A("GBt"), [[16, 8], [0, 16]], O.is_ge, 15, -1)
    AFF(A("ID"), A("GB"), [[-1, 128]], O.is_equal, 0, 1)
    MS(A("WSA"), 0.0)
    for n, c in enumerate((-4080.0, 383.0 * BIG, 255.0, -1.0, 97.0)):
        MS(A("CB", n, n + 1), c)
    TS(A("pi2"), A("pi"), 15, None, O.bitwise_and)
    TC(A("PI"), A("pi2"))
    TC(A("wtf"), A("wti"))
    TC(A("kmf"), A("kmi"))
    TS(A("gwA"), A("GB", 0, 128, 16), A("wtf", 0, 1), None, O.mult)
    MS(A("SEL"), 0.0)

    def spread(dst, src, step):
        for h in range(8):
            ACT(A(dst, 16 * h, 16 * h + 129 * 15 + 1, 129), A("oneb", 0, 16), CP, scale=A(src, step * h, step * h + 1))
    spread("WSA", "gwA", 1)

    def lists(r):
        G, WS = "G%d" % (r % 2), ("WSA", "WSB")[r % 2]
        for i in range(16):
            MM(A("pA", 0, 64), A(WS, 128 * i, 128 * i + 128), A(G, i, S, 16), i == 0, i == 15)
        TC(A("Ui"), A("pA", 0, 64))
        TS(A("Um"), A("Ui"), 4095, None, O.bitwise_and)
        TC(A("Uf"), A("Um"))
        for m in range(M):
            ACT(A(("pB", "pM")[m // 4], 64 * (m % 4), 64 * (m % 4) + 64), A("Uf"), CP, scale=A("kmf", m, m + 1))
        TT(A("UU"), A("Um"), A("Um"), O.mult)
        TS(A("FQ"), A("UU"), 5, None, O.arith_shift_right)
        for h in range(2):
            for m in range(4 * h, 4 * h + 4):
                TT(A("CA", 64 * m, 64 * m + 64), A(("pB", "pM")[h], 64 * (m % 4), 64 * (m % 4) + 64), A("FQ"), O.add)
            TS(A("C", 256 * h, 256 * h + 256), A("CA", 256 * h, 256 * h + 256), W - 1, None, O.bitwise_and)
            TC(A("OFF", 256 * h, 256 * h + 256), A("C", 256 * h, 256 * h + 256))
            if h == 0 and r:
                ACT(A("XG"), IND(A("X"), A("OFF", 0, 64)), CP)
                ACT(A("XH"), IND(A("X"), A("OFF", 96, 128)), CP)

    KB4 = ("pK0", "pK1", "pN", "pM")

    def scores(r):
        G = "G%d" % (r % 2)
        for h in range(2):
            MM(A("pD%d" % h), A("IDb"), A("XG", 512 * h, 512 * h + 512), True, False)
            MM(A("pD%d" % h), A("IDb"), A(G, 512 * h, 512 * h + 512), False, True)
        MM(A("pA"), A("IDb"), A("XH"), True, False)
        MM(A("pA"), A("IDb"), A(G, 512, S), False, True)

        def flag(h):
            TS(A("FL", 256 * h, 256 * h + 256), A("C", 256 * h, 256 * h + 256), W - 96, None, O.is_ge)

        def keys(m):
            k = KB4[m % 4]
            for i in range(16):
                MM(A(k, 0, 64), A("SEL", 128 * i, 128 * i + 128), A("A%d" % (m % 3), i, S, 16), i == 0, False)
            MM(A(k, 0, 64), A("IDb"), A("FL", 64 * m, 64 * m + 64), False, m == 0)
            if m:
                MM(A(k, 0, 64), A("IDb"), A("M2C", 64 * m, 64 * m + 64), False, True)

        def least(m):
            if m == 0:
                TC(A("KM"), A(KB4[0], 0, 64))
            elif m > 0:
                TT(A("KM"), A(KB4[m % 4], 0, 64), A("KM"), O.min)
        for h in range(2):
            ACT(A("A0", 512 * h, 512 * h + 512), A("pD%d" % h), AF.Abs, bias=A("CB", 0, 1), scale=16.0)
        ACT(A("A1", 512, S), A("pA"), AF.Abs, bias=A("CB", 0, 1), scale=16.0)
        for m in range(1, M):
            for h in range(2 if m == M - 1 else 1):
                n = S // 2 if m in (1, M - 1) else S
                a, b = n * h, n * h + n
                TT(A("D%d" % (m % 3), a, b), IND(A("X"), A("OFF", 64 * m + a // 16, 64 * m + b // 16)), A(G, a, b), O.add)
                ACT(A("A%d" % (m % 3), a, b), A("D%d" % (m % 3), a, b), AF.Abs, bias=A("CB", 0, 1), scale=16.0)
            if m == 5 and r == 0:
                ACT(A("NO"), A("X0"), RL, bias=A("CB", 1, 2), scale=-2 * BIG)
            if m == 1:
                flag(0)
                keys(0)
            if m == 3:
                flag(1)
            keys(m)
            least(m - 3)
        least(M - 3)
        least(M - 2)
        utable(0)
        if r:
            TC(IND(A("FW"), A("ROu")), A("ZR"))
        least(M - 1)

    def wrap(dst, src, tmp):
        TT(A(tmp), src, A("MW"), O.mult)
        SCAN(A(dst), A("RST"), A(tmp), 0.0, O.mult, O.add)

    def utable(k):
        if k == 0:
            SCAN(A("UL", s=-1), A("NO", s=-1), A("PL", s=-1), float(W + 1), O.min, O.max)
            TS(A("OF"), A("I16"), A("UL", 0, 1), None, O.mult)
            MM(A("pD0", 0, 16), A("GB"), A("OF"), True, True)
        elif k == 1:
            TT(A("FM"), A("pD0", 0, 16), A("LM"), O.max)
        elif k == 2:
            RED(A("UI"), A("FM"), O.min)
        else:
            TS(A("U2"), A("UL"), A("UI"), None, O.min)
            DMA("y", A("FW", 0, W, rows=slice(0, 128, 16)), A("U2"))

    lists(0)
    IOTA(A("QM"), [[0, 6], [1, 16]], 0, 0)
    AFF(A("B0"), A("GB"), [[-16, 8], [0, 16]], O.is_equal, 0, 1)
    AFF(A("USf"), A("GB"), [[-1, 128]], O.is_gt, 0, 1)
    IOTA(A("PL0"), [[1, 512]], 2, 0)
    IOTA(A("QB0"), [[16, 6]], 0, 0)
    IOTA(A("BI"), [[1, 64]], 0, 0)
    IOTA(A("i16"), [[1, 16]], 0, 0)
    IOTA(A("it0"), [[0, 8], [1, 16]], 1, 0)
    for n, c, base in (("Q0", 96, 0), ("Q1", 96, 1), ("QT", 96, W + CAP + 1), ("ib", 64, 0)):
        IOTA(A(n), [[1, c]], base, 0)
    IOTA(A("SLh"), [[16, 64]], 0, 0)
    IOTA(A("M2C"), [[2, 8], [0, 64]], 0, 0)
    IOTA(A("FW"), [[0, FWW]], 0, 0)
    for n, c, base in (("KD", 72, 0), ("PW", 72, -1), ("LWn", 72, 0), ("HX", 72, 0), ("ZR", 96, 0), ("NEG", 512, -1), ("WSB", 2048, 0), ("SI0", 8, 0), ("SI1", 8, 0), ("SI2", 8, 0)):
        IOTA(A(n), [[0, c]], base, 0)
    for n, a, b in (("GQ", 96, 112), ("SPQ", 96, 112), ("STQ", 192, 208)):
        IOTA(A(n, a, b), [[0, 16]], 0, 0)
    spread("SEL", "GB", 16)
    for n, a, c in (("IDb", "ID", 1.0), ("GBb", "GB", 1.0), ("nUS", "USf", -1.0), ("GB32", "GB", 32.0), ("GB8", "GB", 8.0), ("IDB", "ID", BIG)):
        ACT(A(n), A(a), CP, scale=c)
    ACT(A("XG"), IND(A("X"), A("OFF", 0, 64)), CP)
    ACT(A("XH"), IND(A("X"), A("OFF", 96, 128)), CP)
    TS(A("th16"), A("thi"), 16.0, None, O.mult)
    TS(A("P512"), A("PI"), 512.0, None, O.mult)
    TS(A("P513"), A("PI"), 512.0, 1.0, O.mult, O.add)
    TS(A("P5K"), A("P513"), 10000.0, None, O.mult)
    TS(A("PL"), A("PL0"), A("P512"), None, O.add)
    TS(A("MW"), A("QM"), A("PI"), None, O.is_equal)
    TS(A("NMW"), A("MW"), -1.0, None, O.mult)
    TS(A("RST"), A("QM"), 0.0, None, O.is_gt)
    TS(A("QB"), A("QB0"), A("PI"), 0.5, O.add, O.add)
    TS(A("QBK"), A("QB"), -97.0, None, O.add)
    TS(A("CB", 5, 6), A("PI"), 1.0 / 1024, None, O.mult)
    TS(A("BI"), A("BI"), 1.0 / 32, A("CB", 5, 6), O.mult, O.add)
    TS(A("I16"), A("i16"), A("PI"), None, O.is_equal)
    TS(A("LM"), A("i16"), A("PI"), BIG, O.is_le, O.mult)
    TS(A("SLi"), A("oneb", 0, 64), A("PI"), None, O.mult)
    TS(A("SLf"), A("SLh"), A("PI"), None, O.add)
    TT(A("it1"), A("it0"), A("GB"), O.mult)
    TS(A("IT2"), A("it1"), -1.0, None, O.add)
    TS(A("gwB"), A("GB", 0, 128, 16), A("wtf", 1, 2), None, O.mult)
    TS(A("gwA"), A("GB", 0, 128, 16), A("wtf", 2, 3), None, O.mult)

    near, far = T.cores[rank ^ 1], T.cores[rank ^ 2]

    def to(dst, eng, sem, src, out):
        rid, pid = topo.addr(dst)[0:2]
        return RemoteDMATransfer(dst_ids=[DstId(rid=rid, pnc=pid)], dma_engine_mask=sum(1 << e for e in eng), remote_sem=T.sem[sem], src=src[0], dst=out[0])
    en, ef = topo.engines(core, near), topo.engines(core, far)
    hn = len(en) // 2

    for r in range(RO):
        last = r == RO - 1
        G, H = "G%d" % (r % 2), "G%d" % ((r + 1) % 2)
        SI, SP, STn, RI, RJ, Z, SG = ("%s%d" % (n, r) for n in ("SI", "SP", "ST", "RI", "RJ", "Z", "SG"))
        if r:
            lists(r)
        scores(r)
        if r == 0:
            for n, a, c in (("nB02", "B0", -2.0), ("nIDBb", "ID", -BIG), ("nIDb", "ID", -1.0), ("GBK", "GB", BIG), ("IDK", "ID", BIG),
                            ("ID2b", "ID", 2.0), ("ID3b", "ID", 3.0)):
                ACT(A(n), A(a), CP, scale=c)
        TC(A("KMi"), A("KM"))
        TS(A("F0"), A("KM"), A("th16"), None, O.is_lt)
        utable(1)
        TS(A("PAR"), A("KMi"), 1, None, O.bitwise_and)
        TS(A("MX"), A("KMi"), 14, None, O.bitwise_and)
        TT(A("FIT"), A("F0"), A("PAR"), O.is_gt)
        utable(2)
        TS(A("KD", 0, 64), A("KMi"), 65520, None, O.bitwise_and)
        SCAN(A("CS"), A("one", 0, 64), A("FIT"), 0.0, O.mult, O.add)
        MM(A("pB", 0, 64), A("GBb"), A("CS"), True, True)
        MM(A("pM", 0, 64), A("GBb"), A("CS"), True, False)
        MM(A("pM", 0, 64), A("nUS"), A("FIT"), False, True)
        MM(A("pN", 0, 64), A("GBb"), A("CS"), True, True)
        for a in range(6):
            ACT(A("JK", 64 * a, 64 * a + 64), A("pB", 0, 64), AF.Sign, bias=A("QB", a, a + 1), scale=-1.0, acc=A("BQ", a, a + 1))
        if last:
            MM(A("pK1"), A("IDb"), A("SG1"), True, False)
            MM(A("pK1"), A("nIDb"), A("SG0"), False, True)
            ACT(A("N1"), A("pK1"), RL)
        if not last:
            spread(("WSB", "WSA")[r], ("gwB", "gwA")[r], 1)
        utable(3)
        TT(A("LWn", 0, 64), A("MX"), A("BI"), O.add)
        TT(A("PW", 0, 64), A("pM", 0, 64), A("FIT"), O.mult)
        TS(A("INVb"), A("Q0"), A("pN", 63, 64), None, O.is_ge)
        TS(A("INV"), A("INVb"), 2.0 ** -14, None, O.add)
        TS(A("BQo"), A("BQ"), 0.5, 32.0, O.mult, O.add)
        TT(A("OH"), IND(A("PW"), A("BQo")), A("Q1"), O.is_equal)
        TT(A("LG"), IND(A("LWn"), A("BQo")), A("OH"), O.mult)
        MM(A("pA", 0, 96), A("GB32"), A("LG"), True, True)
        TT(A("KG"), IND(A("KD"), A("BQo")), A("OH"), O.mult)
        MM(A("pK0", 0, 96), A("GB8"), A("KG"), True, False)
        MM(A("pK0", 0, 96), A("ID"), A("Q0"), False, True)
        TS(A("T1"), A("BQ"), 8.0, 608.0, O.mult, O.add)
        wrap("SL", A("pA", 0, 96), "WL")
        TC(A("LO"), A("SL", *q6))
        TT(A("WK"), A("pK0", 0, 96), A("NMW"), O.mult)
        TT(A("CG"), IND(A("C"), A("LO")), A("OH"), O.mult)
        MM(A("pA", 0, 96), A("GB"), A("CG"), True, False)
        MM(A("pA", 0, 96), A("IDB"), A("INV"), False, True)
        SCAN(A("SK"), A("RST"), A("WK"), 0.0, O.mult, O.add)
        for a in range(6):
            ACT(A("SGN", 96 * a, 96 * a + 96), A("pK0", 0, 96), AF.Sign, bias=A("SK", 16 * a + 15, 16 * a + 16))
        TS(A("XA"), A("SL", *q6), 32.0, None, O.mult)
        wrap("SC", A("pA", 0, 96), "WC")
        for a in range(6):
            ACT(A("KB", 96 * a, 96 * a + 96), A("SGN", 96 * a, 96 * a + 96), CP, scale=A("SC", 16 * a + 15, 16 * a + 16))
        TS(A("UO"), A("SC", *q6), 15.0, W - 1.0, O.add, O.min)
        TS(A("XI"), A("XA"), 2047, None, O.bitwise_and)
        TC(A("EG"), IND(A("FW"), A("UO")))
        MM(A("pM", 0, 96), A("B0"), A("EG"), True, True)
        TT(A("T2"), A("XI"), A("T1"), O.subtract)
        TS(A("PO"), A("SC", *q6), 9.0, W - 1.0, O.add, O.min)

        def same(a):
            TT(A("KL", 96 * a, 96 * a + 96), A("KB", 96 * a, 96 * a + 96), A("pA", 0, 96), O.is_equal)
            MM(A("pK1", 0, 96), A("GBK"), A("KL", 96 * a, 96 * a + 96), a == 0, False)
        TS(A("SQ"), A("T2"), 96.0, None, O.add)
        TS(A("C6"), A("SC", *q6), -1.0, W - 1.0, O.add, O.min)
        wrap("S1", A("pM", 0, 96), "W1")
        TS(A("UO2"), A("S1", *q6), 6.0, W - 1.0, O.add, O.min)
        TC(A("EG2"), IND(A("FW"), A("UO2")))
        MM(A("pN", 0, 96), A("B0"), A("EG2"), True, True)
        ACT(A("PG"), IND(A("X"), A("PO")), CP)
        ACT(A("PN"), A("PG"), RL, scale=-1.0)
        MM(A("pD0", 0, 96), A("nIDb"), A("PG"), True, False)
        MM(A("pD0", 0, 96), A("nB02"), A("PN"), False, True)
        for a in range(4):
            same(a)
        TT(A("W2"), A("pN", 0, 96), A("MW"), O.mult)
        same(4)
        SCAN(A("S2"), A("RST"), A("W2"), 0.0, O.mult, O.add)
        same(5)
        MM(A("pK1", 0, 96), A("IDK"), A("INVb"), False, True)
        TS(A("TO", 0, 6), A("S1", *q6), -2.0, None, O.add)
        TS(A("TO", 6, 12), A("S2", *q6), -2.0, None, O.add)
        ACT(A("CR"), A("pA", 0, 96), CP)
        ACT(A("M1"), A("CR"), RL, bias=A("P5K"), scale=-10000.0)
        ACT(A("SPQ", 0, 96), A("pD0", 0, 96), RL, bias=A("CB", 2, 3))
        ACT(A("TG"), IND(A("X"), A("TO")), CP)
        ACT(A("TN"), A("TG"), RL, scale=-1.0)
        MM(A("pD1", 0, 192), A("nIDb"), A("TG"), True, False)
        MM(A("pD1", 0, 192), A("nB02"), A("TN"), False, True)
        TT(A("NCQ"), A("pK1", 0, 96), A("QT"), O.min)
        TS(A("CUT"), A("NCQ"), 0.5, None, O.is_lt)
        SCAN(A("RK"), A("one", 0, 96), A("CUT"), -97.0, O.mult, O.add)
        ACT(A(SI, 0, 1), A("RK", 95, 96), AF.Identity, bias=A("CB", 4, 5))
        ACT(A(SI, 7, 8), A("RK", 95, 96), AF.Identity, bias=A("CB", 3, 4), scale=-1.0)
        SEND([A(SI)], 2 * hn, lambda: g.remote_dma_fused([to(near, en[:hn], "ai%d" % r, A(SI), A(RI)), to(far, ef[hn:], "aj%d" % r, A(SI), A(RJ))], local_sem=T.sem["loc"]))
        for a in range(6):
            ACT(A("JL", 96 * a, 96 * a + 96), A("RK"), AF.Sign, bias=A("QBK", a, a + 1), scale=-1.0, acc=A("BK", a, a + 1))
        ACT(A("STQ", 0, 192), A("pD1", 0, 192), RL, bias=A("CB", 2, 3))
        TT(A("CD"), A("NCQ"), A("RK"), O.add)
        TT(A("LEN"), A("pN", 0, 96), A("CR"), O.subtract)
        TT(A("WD"), A("CD"), A("MW"), O.mult)
        SCAN(A("SD"), A("RST"), A("WD"), 0.0, O.mult, O.add)
        TT(A("R6"), A("C6"), A("SD", *q6), O.max)
        TT(A("VV"), A("T2"), A("SD", *q6), O.subtract)
        TS(A("KIu", 0, 6), A("BK"), 0.5, 48.0, O.mult, O.add)
        TS(A("KIu", 6, 12), A("BK"), 0.5, 144.0, O.mult, O.add)
        ACT(A(SP), IND(A("SPQ"), A("KIu", 0, 6)), CP)
        SEND([A(SP)], len(en), lambda: g.remote_dma_fused([to(near, en, "ap%d" % r, A(SP), A(Z, 0, 96))], local_sem=T.sem["loc"]))
        ACT(A(STn), IND(A("STQ"), A("KIu")), CP)
        SEND([A(STn)], len(ef), lambda: g.remote_dma_fused([to(far, ef, "at%d" % r, A(STn), A(Z, 96, 288))], local_sem=T.sem["loc"]))
        ACT(A("GQ", 0, 96), IND(A(G, 0, S), A("SQ")), CP)
        ACT(A(G, S, S + CAP), IND(A("GQ"), A("KIu", 0, 6)), CP)
        TC(A("ROu"), A("R6"))
        TS(A("BII", 0, 6), A("VV"), 16383, 4, O.bitwise_and, O.arith_shift_right)
        TS(A("BII", 6, 12), A("VV"), 15, None, O.bitwise_and)
        LAND(A(RI), "ai%d" % r, hn)
        LAND(A(RJ), "aj%d" % r, len(ef) - hn)
        LAND(A(Z, 0, 96), "ap%d" % r, len(en))
        LAND(A(Z, 96, 288), "at%d" % r, len(ef))
        TC(IND(A("FW"), A("ROu")), A("LEN"))
        DMA("y", A("LW"), A("FW", 0, W, rows=slice(1, 128, 16)))
        TC(A("BIF"), A("BII"))
        for a in range(6):
            ACT(A("EA", 64 * a, 64 * a + 64), A("ib"), AF.Abs, bias=A("BIF", a, a + 1), scale=-1.0)
        ACT(A("EB"), A("EA"), RL, bias=A("one", 0, 1), scale=-1.0)
        for a in range(6):
            TS(A("TA", 128 * a, 128 * a + 128), A("IT2"), A("BIF", 6 + a, 7 + a), None, O.is_ge)
            if a == 1:
                TT(A("M2"), A("pN", 0, 96), A("M1"), O.min)
            if a == 3:
                RED(A("RD"), A("M2"), O.max)
        TS(A("IN"), A("RD"), A("P512"), 0.0, O.subtract, O.max)
        for a in range(6):
            MM(A("pB", 0, 64), A("GBb"), A("EB", 64 * a, 64 * a + 64), a == 0, a == 5)
        MM(A("pA", 0, 64), A("IDb"), A("SLh"), True, False)
        MM(A("pA", 0, 64), A("IDb"), A("SLi"), False, False)
        for a in range(6):
            MM(A("pA", 0, 64), A("TA", 128 * a, 128 * a + 128), A("EB", 64 * a, 64 * a + 64), False, a == 5)
        SCAN(A("HX", 1, 65), A("one", 0, 64), A("pB", 0, 64), 0.0, O.mult, O.add)
        TT(A("IX"), A("pA", 0, 64), A("HX", 0, 64), O.add)
        TC(A("IXu"), A("IX"))
        ACT(A(Z, 288, 288 + S), IND(A(G, 0, S + CAP), A("IXu")), CP)
        TT(A("NT1"), A(RI, 0, 1), A(RJ, 0, 1), O.add)
        TS(A("F1"), A("SLf"), A(RI, 0, 1), A(RI, 7, 8), O.is_ge, O.mult)
        TT(A("NT2"), A("NT1"), A(RJ, 0, 1), O.add)
        TS(A("F2"), A("SLf"), A("NT1"), A(RJ, 7, 8), O.is_ge, O.mult)
        TS(A("F3"), A("SLf"), A("NT2"), A(RJ, 7, 8), O.is_ge, O.mult)
        SCAN(A("ST"), A("NEG"), A("LW"), A("IN"), O.add, O.max)
        ACT(A(SG), A("ST"), AF.Sign)
        for k, n in enumerate(("SLh", "SLi", "F1", "F2", "F3")):
            MM(A("pM", 0, 64), A("IDb"), A(n), k == 0, k == 4)
        if not last:
            MM(A("pK0"), A("IDb"), A("X0"), True, False)
            MM(A("pK0"), A("nIDBb"), A(SG), False, True)
        TC(A("FX"), A("pM", 0, 64))
        TC(A(H, 0, S // 2), IND(A(Z), A("FX", 0, 32)))
        ACT(A(H, S // 2, S), IND(A(Z), A("FX", 32, 64)), CP)
        if last:
            DMA("y", XT(T.yg[:, :]), A(H, 0, S))
        else:
            TC(A("X0"), A("pK0"))
            ACT(A("NO"), A("X0"), RL, bias=A("CB", 1, 2), scale=-2 * BIG)
            DMA("y", A("X", 0, W, rows=slice(0, 128, 16)), A("X0"))
        if last:
            MM(A("pK1"), A("IDb"), A(SG), True, False)
            MM(A("pK1"), A("nIDb"), A("SG0"), False, False)
            MM(A("pK1"), A("nIDb"), A("N1"), False, True)
            ACT(A("N2"), A("pK1"), RL)
            MM(A("pD0"), A("IDb"), A("SG0"), True, False)
            MM(A("pD0"), A("ID2b"), A("N1"), False, False)
            MM(A("pD0"), A("ID3b"), A("N2"), False, True)
            ACT(A("YC"), A("pD0"), CP)
            DMA("s", XT(T.yc[:, :]), A("YC"))
    END()
